import numpy as np
import ml_dtypes


def mxq(x, axis, fmt="e4m3"):
    dtype, down = {"e4m3": (ml_dtypes.float8_e4m3fn, 7), "e5m2": (ml_dtypes.float8_e5m2, 14)}[fmt]
    v = np.moveaxis(np.asarray(x, np.float32).astype(ml_dtypes.bfloat16).astype(np.float64), axis, -1)
    blocks = v.reshape(v.shape[:-1] + (-1, 32))
    amax = np.abs(blocks).max(-1, keepdims=True)
    byte = np.maximum(np.where(amax > 0, np.frexp(amax)[1] - 1 + 127, 0) - down, 1)
    scale = np.exp2(byte - 127.0)
    codes = (blocks / scale).astype(np.float32).astype(dtype).astype(np.float64)
    return np.moveaxis((codes * scale).reshape(v.shape), -1, axis)


WIDE = False


def mx_kscale(k):
    if not WIDE:
        return np.ones(k)
    levels = np.array([10, -10, 5, -5, 0])
    if k % 512:
        return np.exp2(np.random.permutation(np.resize(levels, k // 32))).repeat(32)
    a = np.empty((k // 512, 16))
    for p in range(k // 512):
        a[p, :8] = np.random.permutation(np.resize(levels, 8))
        for g in range(8):
            far = levels[np.abs(levels - a[p, g]) >= 10]
            a[p, g + 8] = far[np.random.randint(len(far))]
    return np.exp2(a.ravel()).repeat(32)


def f64(x):
    return np.asarray(x).astype(np.float64)


def striped(idx):
    return np.tile(idx.reshape(-1, 16).T, (8, 1)).astype(np.uint16)


def unstriped(offs):
    return offs[:16].T.reshape(-1).astype(np.int64)


E2M1 = np.array([0.0, 0.5, 1.0, 1.5, 2.0, 3.0, 4.0, 6.0, -0.0, -0.5, -1.0, -1.5, -2.0, -3.0, -4.0, -6.0])


def pack_weight(w, fmt):
    k, n = w.shape
    w = f64(np.asarray(w, np.float32).astype(ml_dtypes.bfloat16)).reshape(k // 32, 32, n)
    amax = np.abs(w).max(1)
    if fmt == "e4m3":
        byte = np.frexp(amax)[1] - 1 + 127 - 7
    else:
        mant, ex = np.frexp(amax / 6.0)
        byte = np.where(mant > 0.5, ex, ex - 1) + 127
    byte = np.clip(np.where(amax > 0, byte, 1), 1, 254)
    scaled = (w * np.exp2(127.0 - byte)[:, None, :]).reshape(k, n).astype(np.float32)
    by_word = np.ascontiguousarray(scaled.reshape(k // 512, 128, 4, n).transpose(0, 1, 3, 2))
    if fmt == "e4m3":
        words = by_word.astype(ml_dtypes.float8_e4m3fn).view(np.uint8)
    else:
        c = by_word.astype(ml_dtypes.float4_e2m1fn).view(np.uint8) & 0xF
        words = (c[..., 0::2] | (c[..., 1::2] << 4)).reshape(k // 512, 128, 2 * n)
    return np.ascontiguousarray(words), np.ascontiguousarray(byte.astype(np.uint8).reshape(k // 512, 16, n))


def unpack_weight(words, scales, fmt):
    g, _, n = scales.shape
    words = np.ascontiguousarray(words).reshape(g, 128, n, -1)
    if fmt == "e4m3":
        vals = words.view(ml_dtypes.float8_e4m3fn).astype(np.float64)
    else:
        nib = np.empty((g, 128, n, 4), np.uint8)
        nib[..., 0::2] = words & 0xF
        nib[..., 1::2] = words >> 4
        vals = E2M1[nib]
    vals = vals * np.repeat(np.exp2(scales.astype(np.float64) - 127.0), 8, axis=1)[..., None]
    return vals.transpose(0, 1, 3, 2).reshape(g * 512, n)


def gelu(v):
    return 0.5 * v * (1.0 + np.tanh(np.sqrt(2.0 / np.pi) * (v + 0.044715 * v**3)))


K, H, N, T, S = 1024, 1536, 384, 2048, 512

def setup_inputs():
    n = np.random.standard_normal
    s = mx_kscale(K)[:, None]
    u = mx_kscale(H)[:, None]
    tab_words, tab_scales = pack_weight(n((K, T)) * s, "e2m1")
    wa_words, wa_scales = pack_weight(n((K, H)) / np.sqrt(K) / s, "e4m3")
    wr_words, wr_scales = pack_weight(n((H, N)) / np.sqrt(H) / u, "e2m1")
    return {
        "tab_words": tab_words, "tab_scales": tab_scales,
        "offs": striped(np.random.permutation(T)[:S]),
        "offs2": striped(np.random.permutation(T)[:S]),
        "wo": (n((K, H)) / np.sqrt(K) / s * u.T).astype(np.float32),
        "wa_words": wa_words, "wa_scales": wa_scales,
        "rel": n((H, S)).astype(np.float32),
        "wr_words": wr_words, "wr_scales": wr_scales,
    }

def reference(tab_words, tab_scales, offs, offs2, wo, wa_words, wa_scales, rel, wr_words, wr_scales):
    TW = unpack_weight(tab_words, tab_scales, "e2m1")
    v = TW[:, unstriped(offs)]
    v2 = TW[:, unstriped(offs2)]
    a = mxq(f64(wo), 0, "e4m3").T @ v
    b = unpack_weight(wa_words, wa_scales, "e4m3").T @ v2
    h = a * b * f64(rel)
    hq = mxq(h, 0, "e4m3")
    return unpack_weight(wr_words, wr_scales, "e2m1").T @ hq

@@ -1,0 +1,235 @@
+from contextlib import ExitStack
+
+import concourse.mybir as mybir
+
+K, H, N, T, S = 1024, 1536, 384, 2048, 512
+FLOPS = 2 * (2 * K * H * S + H * N * S)
+
+F32 = mybir.dt.float32
+BF16 = mybir.dt.bfloat16
+I32 = mybir.dt.int32
+U16 = mybir.dt.uint16
+U8 = mybir.dt.uint8
+FP8X4 = mybir.dt.float8_e4m3fn_x4
+FP4X4 = mybir.dt.float4_e2m1fn_x4
+MULT = mybir.AluOpType.mult
+
+P = 128
+PACK = 4
+K_PASS = P * PACK
+PASSES = K // K_PASS
+BLOCKS = H // K_PASS
+QUADS = 4
+ROWS = 4
+JQ = S // P
+N_TILES = N // P
+HALF = K_PASS // 2
+MOVED = 3 * 32 + ROWS
+
+
+def tile_list_provenance_claim_readout_kernel(
+    tc, tab_words, tab_scales, offs, offs2, wo, wa_words, wa_scales, rel, wr_words, wr_scales, out
+):
+    nc = tc.nc
+    with ExitStack() as ctx:
+        keep = ctx.enter_context(tc.tile_pool(name="keep", bufs=1))
+        work = ctx.enter_context(tc.psum_pool(name="work", bufs=4))
+        sums = ctx.enter_context(tc.psum_pool(name="sums", bufs=1))
+
+        def tile(shape, dtype, name):
+            return keep.tile(shape, dtype, name=name, align_bytes=64)
+
+        own_list = keep.tile([P, S // 16], U16, name="own_list")
+        art_list = keep.tile([P, S // 16], U16, name="art_list")
+        tab_w = [tile([P, T], U16, f"tab_w{a}") for a in range(PASSES)]
+        tab_s = tile([P, T], U8, "tab_s")
+        wa_s_raw = tile([P, H], U8, "wa_s_raw")
+        wa_s = [tile([P, H], U8, f"wa_s{a}") for a in range(PASSES)]
+        v_s = [tile([P, 2 * S], U8, f"v_s{a}") for a in range(PASSES)]
+        wr_w = tile([P, BLOCKS, 2 * N], U8, "wr_w")
+        wr_s = tile([P, BLOCKS, N], U8, "wr_s")
+
+        nc.vector.memset(tab_s[:].bitcast(I32), 0)
+        nc.vector.memset(wa_s_raw[:].bitcast(I32), 0)
+        nc.vector.memset(v_s[1][:].bitcast(I32), 0)
+        nc.vector.memset(wa_s[1][:].bitcast(I32), 0)
+        nc.vector.memset(wr_s[:].rearrange("p a c -> p (a c)").bitcast(I32), 0)
+
+        nc.sync.dma_start(art_list[:], offs2)
+        nc.sync.dma_start(own_list[:], offs)
+        for q in range(QUADS):
+            nc.scalar.dma_start(
+                out=tab_s[32 * q : 32 * q + PASSES * ROWS, :].bitcast(I32),
+                in_=tab_scales[:, ROWS * q : ROWS * (q + 1), :].bitcast(I32),
+            )
+        for a in range(PASSES):
+            nc.sync.dma_start(out=tab_w[a][:].bitcast(I32), in_=tab_words[a].bitcast(I32))
+
+        wo_raw = {}
+        wa_raw = {}
+        rel_sb = {}
+
+        def load_wo(b, a):
+            rows = wo[a * K_PASS : (a + 1) * K_PASS, :].rearrange("(p j) c -> p j c", j=PACK)
+            for h in range(2):
+                wo_raw[b, a, h] = tile([P, PACK, HALF], F32, f"wo_raw{b}{a}{h}")
+                c0 = b * K_PASS + h * HALF
+                nc.sync.dma_start(out=wo_raw[b, a, h][:], in_=rows[:, :, c0 : c0 + HALF])
+
+        def load_wa(b):
+            wa_raw[b] = tile([P, PASSES, K_PASS], I32, f"wa_raw{b}")
+            words = wa_words.rearrange("a p c i -> p a (c i)").bitcast(I32)
+            nc.sync.dma_start(out=wa_raw[b][:], in_=words[:, :, b * K_PASS : (b + 1) * K_PASS])
+
+        def load_rel(b, h):
+            rows = rel[b * K_PASS : (b + 1) * K_PASS, :].rearrange("(p t) j -> p t j", t=PACK)
+            rel_sb[b, h] = tile([P, 2, S], F32, f"rel{b}{h}")
+            nc.sync.dma_start(out=rel_sb[b, h][:], in_=rows[:, 2 * h : 2 * h + 2, :])
+
+        load_wo(0, 0)
+        for q in range(QUADS):
+            nc.gpsimd.dma_start(
+                out=wa_s_raw[32 * q : 32 * q + PASSES * ROWS, :].bitcast(I32),
+                in_=wa_scales[:, ROWS * q : ROWS * (q + 1), :].bitcast(I32),
+            )
+        load_wo(0, 1)
+        load_wa(0)
+        load_rel(0, 0)
+        load_rel(0, 1)
+        for b in range(1, BLOCKS):
+            load_wa(b)
+            load_wo(b, 0)
+            load_rel(b, 0)
+            load_wo(b, 1)
+            load_rel(b, 1)
+        nc.sync.dma_start(out=wr_w[:].bitcast(I32), in_=wr_words.rearrange("a p c -> p a c").bitcast(I32))
+
+        nc.vector.tensor_copy(v_s[0][:, 0:S], tab_s[:].indirect(art_list[:]))
+        nc.vector.tensor_copy(v_s[0][:, S : 2 * S], tab_s[:].indirect(own_list[:]))
+        nc.gpsimd.dma_start(out=v_s[1][0:MOVED, :].bitcast(I32), in_=v_s[0][ROWS : ROWS + MOVED, :].bitcast(I32))
+        art_w = [tile([P, S], U16, f"art_w{a}") for a in range(PASSES)]
+        own_w = [tile([P, S], U16, f"own_w{a}") for a in range(PASSES)]
+        nc.vector.tensor_copy(art_w[0][:], tab_w[0][:].indirect(art_list[:]))
+        nc.vector.tensor_copy(
+            wa_s[0][:].rearrange("p (t c) -> p t c", t=PACK), wa_s_raw[:].rearrange("p (c t) -> p t c", t=PACK)
+        )
+        nc.gpsimd.dma_start(out=wa_s[1][0:MOVED, :].bitcast(I32), in_=wa_s[0][ROWS : ROWS + MOVED, :].bitcast(I32))
+        nc.vector.tensor_copy(art_w[1][:], tab_w[1][:].indirect(art_list[:]))
+        for a in range(PASSES):
+            nc.vector.tensor_copy(own_w[a][:], tab_w[a][:].indirect(own_list[:]))
+        for q in range(QUADS):
+            nc.gpsimd.dma_start(
+                out=wr_s[32 * q : 32 * q + ROWS, :, :].bitcast(I32),
+                in_=wr_scales[:, ROWS * q : ROWS * (q + 1), :].rearrange("a r c -> r a c").bitcast(I32),
+            )
+
+        wo_bf = {}
+        wo_w = {}
+        wo_s = {}
+        wa_w = {}
+        b_rel = {}
+        h_bf = {}
+        acc = [sums.tile([P, N_TILES, P], F32, name=f"acc{jq}") for jq in range(JQ)]
+
+        def round_wo(b, a):
+            wo_bf[b, a] = tile([P, PACK, P, PACK], BF16, f"wo_bf{b}{a}")
+            for h in range(2):
+                dst = wo_bf[b, a][:, :, h * (P // 2) : (h + 1) * (P // 2), :]
+                nc.scalar.copy(
+                    out=dst.rearrange("p (u w) m j -> p u m j w", w=2),
+                    in_=wo_raw[b, a, h][:].rearrange("p j (m u w) -> p u m j w", u=2, w=2),
+                )
+
+        def quantise_wo(b, a):
+            wo_w[b, a] = tile([P, K_PASS], I32, f"wo_w{b}{a}")
+            wo_s[b, a] = tile([P, K_PASS], U8, f"wo_s{b}{a}")
+            nc.vector.quantize_mx(
+                out=wo_w[b, a][:].bitcast(FP8X4),
+                scales=wo_s[b, a][:],
+                in_=wo_bf[b, a][:].rearrange("p t m j -> p (t m j)"),
+            )
+
+        def order_wa(b):
+            wa_w[b] = tile([P, PASSES, PACK, P], I32, f"wa_w{b}")
+            nc.vector.tensor_copy(
+                out=wa_w[b][:].rearrange("p a t (c i) -> p a c t i", i=4),
+                in_=wa_raw[b][:].rearrange("p a (c i t) -> p a c t i", i=4, t=PACK),
+            )
+
+        def art_scores(b, t):
+            if t == 0:
+                b_rel[b] = tile([P, PACK, S], F32, f"b_rel{b}")
+            bank = work.tile([P, S], F32, name="bank")
+            c0 = t * (H // PACK) + b * P
+            for a in range(PASSES):
+                nc.tensor.matmul_mx(
+                    out=bank[:],
+                    lhsT=wa_w[b][:, a, t, :].bitcast(FP8X4),
+                    lhsT_scale=wa_s[a][:, c0 : c0 + P],
+                    rhs=art_w[a][:].bitcast(FP4X4),
+                    rhs_scale=v_s[a][:, 0:S],
+                    start=(a == 0),
+                    stop=(a == PASSES - 1),
+                )
+            nc.vector.tensor_tensor(b_rel[b][:, t, :], bank[:], rel_sb[b, t // 2][:, t % 2, :], MULT)
+
+        def own_scores(b, jq):
+            bank = work.tile([P, S], F32, name="bank")
+            cols = slice(jq * P, (jq + 1) * P)
+            for a in range(PASSES):
+                for t in range(PACK):
+                    nc.tensor.matmul_mx(
+                        out=bank[:, t * P : (t + 1) * P],
+                        lhsT=wo_w[b, a][:, t * P : (t + 1) * P].bitcast(FP8X4),
+                        lhsT_scale=wo_s[b, a][:, t * P : (t + 1) * P],
+                        rhs=own_w[a][:, cols].bitcast(FP4X4),
+                        rhs_scale=v_s[a][:, S + jq * P : S + (jq + 1) * P],
+                        start=(a == 0 and t == 0),
+                        stop=(a == PASSES - 1 and t == PACK - 1),
+                    )
+            h_bf[b, jq] = tile([P, P, PACK], BF16, f"h_bf{b}{jq}")
+            nc.vector.tensor_tensor(
+                h_bf[b, jq][:].rearrange("p (c i) t -> p c t i", i=4),
+                bank[:].rearrange("p (t c i) -> p c t i", t=PACK, i=4),
+                b_rel[b][:, :, cols].rearrange("p t (c i) -> p c t i", i=4),
+                MULT,
+            )
+
+        def readout(b, jq):
+            h_w = tile([P, P], I32, f"h_w{b}{jq}")
+            h_s = tile([P, P], U8, f"h_s{b}{jq}")
+            nc.vector.quantize_mx(
+                out=h_w[:].bitcast(FP8X4), scales=h_s[:], in_=h_bf[b, jq][:].rearrange("p j t -> p (j t)")
+            )
+            for n in range(N_TILES):
+                nc.tensor.matmul_mx(
+                    out=acc[jq][:, n, :],
+                    lhsT=wr_w[:, b, 2 * P * n : 2 * P * (n + 1)].bitcast(FP4X4),
+                    lhsT_scale=wr_s[:, b, P * n : P * (n + 1)],
+                    rhs=h_w[:].bitcast(FP8X4),
+                    rhs_scale=h_s[:],
+                    start=(b == 0 and n == 0),
+                    stop=(b == BLOCKS - 1 and n == N_TILES - 1),
+                )
+            if b == BLOCKS - 1:
+                result = tile([P, N_TILES, P], F32, f"result{jq}")
+                nc.scalar.copy(out=result[:], in_=acc[jq][:])
+                nc.sync.dma_start(
+                    out=out[:, jq * P : (jq + 1) * P].rearrange("(n p) j -> p n j", p=P), in_=result[:]
+                )
+
+        for b in range(BLOCKS):
+            round_wo(b, 0)
+            round_wo(b, 1)
+            order_wa(b)
+            quantise_wo(b, 0)
+            art_scores(b, 0)
+            art_scores(b, 1)
+            quantise_wo(b, 1)
+            art_scores(b, 2)
+            art_scores(b, 3)
+            for jq in range(JQ):
+                own_scores(b, jq)
+                if jq > 0:
+                    readout(b, jq - 1)
+            readout(b, JQ - 1)

@@ -24,7 +24,7 @@ ROWS = 4
 JQ = S // P
 N_TILES = N // P
 HALF = K_PASS // 2
-MOVED = 3 * 32 + ROWS
+SHIFT = 16
 
 
 def tile_list_provenance_claim_readout_kernel(
@@ -43,27 +43,32 @@ def tile_list_provenance_claim_readout_kernel(
         art_list = keep.tile([P, S // 16], U16, name="art_list")
         tab_w = [tile([P, T], U16, f"tab_w{a}") for a in range(PASSES)]
         tab_s = tile([P, T], U8, "tab_s")
-        wa_s_raw = tile([P, H], U8, "wa_s_raw")
-        wa_s = [tile([P, H], U8, f"wa_s{a}") for a in range(PASSES)]
         v_s = [tile([P, 2 * S], U8, f"v_s{a}") for a in range(PASSES)]
+        wa_s_raw = tile([P, PASSES, H], U8, "wa_s_raw")
         wr_w = tile([P, BLOCKS, 2 * N], U8, "wr_w")
         wr_s = tile([P, BLOCKS, N], U8, "wr_s")
 
         nc.vector.memset(tab_s[:].bitcast(I32), 0)
-        nc.vector.memset(wa_s_raw[:].bitcast(I32), 0)
+        nc.vector.memset(wa_s_raw[:].rearrange("p a c -> p (a c)").bitcast(I32), 0)
         nc.vector.memset(v_s[1][:].bitcast(I32), 0)
-        nc.vector.memset(wa_s[1][:].bitcast(I32), 0)
         nc.vector.memset(wr_s[:].rearrange("p a c -> p (a c)").bitcast(I32), 0)
+
+        def load_scales(plane, scales):
+            for q in range(QUADS):
+                nc.sync.dma_start(
+                    out=plane[32 * q : 32 * q + ROWS, :, :].bitcast(I32),
+                    in_=scales[:, ROWS * q : ROWS * (q + 1), :].rearrange("a r c -> r a c").bitcast(I32),
+                )
 
         nc.sync.dma_start(art_list[:], offs2)
         nc.sync.dma_start(own_list[:], offs)
-        for q in range(QUADS):
-            nc.scalar.dma_start(
-                out=tab_s[32 * q : 32 * q + PASSES * ROWS, :].bitcast(I32),
-                in_=tab_scales[:, ROWS * q : ROWS * (q + 1), :].bitcast(I32),
+        nc.sync.dma_start(out=tab_w[0][:].bitcast(I32), in_=tab_words[0].bitcast(I32))
+        for r in range(ROWS):
+            nc.sync.dma_start(
+                out=tab_s[r:P:SHIFT, :].bitcast(I32),
+                in_=tab_scales[:, r::ROWS, :].rearrange("a q c -> q a c").bitcast(I32),
             )
-        for a in range(PASSES):
-            nc.sync.dma_start(out=tab_w[a][:].bitcast(I32), in_=tab_words[a].bitcast(I32))
+        nc.sync.dma_start(out=tab_w[1][:].bitcast(I32), in_=tab_words[1].bitcast(I32))
 
         wo_raw = {}
         wa_raw = {}
@@ -87,12 +92,11 @@ def tile_list_provenance_claim_readout_kernel(
             nc.sync.dma_start(out=rel_sb[b, h][:], in_=rows[:, 2 * h : 2 * h + 2, :])
 
         load_wo(0, 0)
-        for q in range(QUADS):
-            nc.gpsimd.dma_start(
-                out=wa_s_raw[32 * q : 32 * q + PASSES * ROWS, :].bitcast(I32),
-                in_=wa_scales[:, ROWS * q : ROWS * (q + 1), :].bitcast(I32),
-            )
         load_wo(0, 1)
+        nc.vector.tensor_copy(v_s[0][:, 0:S], tab_s[:].indirect(art_list[:]))
+        nc.vector.tensor_copy(v_s[0][:, S : 2 * S], tab_s[:].indirect(own_list[:]))
+        nc.sync.dma_start(out=v_s[1][0 : P - SHIFT, :].bitcast(I32), in_=v_s[0][SHIFT:P, :].bitcast(I32))
+        load_scales(wa_s_raw, wa_scales)
         load_wa(0)
         load_rel(0, 0)
         load_rel(0, 1)
@@ -102,27 +106,17 @@ def tile_list_provenance_claim_readout_kernel(
             load_rel(b, 0)
             load_wo(b, 1)
             load_rel(b, 1)
+        load_scales(wr_s, wr_scales)
         nc.sync.dma_start(out=wr_w[:].bitcast(I32), in_=wr_words.rearrange("a p c -> p a c").bitcast(I32))
 
-        nc.vector.tensor_copy(v_s[0][:, 0:S], tab_s[:].indirect(art_list[:]))
-        nc.vector.tensor_copy(v_s[0][:, S : 2 * S], tab_s[:].indirect(own_list[:]))
-        nc.gpsimd.dma_start(out=v_s[1][0:MOVED, :].bitcast(I32), in_=v_s[0][ROWS : ROWS + MOVED, :].bitcast(I32))
         art_w = [tile([P, S], U16, f"art_w{a}") for a in range(PASSES)]
         own_w = [tile([P, S], U16, f"own_w{a}") for a in range(PASSES)]
-        nc.vector.tensor_copy(art_w[0][:], tab_w[0][:].indirect(art_list[:]))
-        nc.vector.tensor_copy(
-            wa_s[0][:].rearrange("p (t c) -> p t c", t=PACK), wa_s_raw[:].rearrange("p (c t) -> p t c", t=PACK)
-        )
-        nc.gpsimd.dma_start(out=wa_s[1][0:MOVED, :].bitcast(I32), in_=wa_s[0][ROWS : ROWS + MOVED, :].bitcast(I32))
-        nc.vector.tensor_copy(art_w[1][:], tab_w[1][:].indirect(art_list[:]))
+        for a in range(PASSES):
+            nc.vector.tensor_copy(art_w[a][:], tab_w[a][:].indirect(art_list[:]))
         for a in range(PASSES):
             nc.vector.tensor_copy(own_w[a][:], tab_w[a][:].indirect(own_list[:]))
-        for q in range(QUADS):
-            nc.gpsimd.dma_start(
-                out=wr_s[32 * q : 32 * q + ROWS, :, :].bitcast(I32),
-                in_=wr_scales[:, ROWS * q : ROWS * (q + 1), :].rearrange("a r c -> r a c").bitcast(I32),
-            )
 
+        wa_s = {}
         wo_bf = {}
         wo_w = {}
         wo_s = {}
@@ -156,16 +150,21 @@ def tile_list_provenance_claim_readout_kernel(
                 in_=wa_raw[b][:].rearrange("p a (c i t) -> p a c t i", i=4, t=PACK),
             )
 
+            wa_s[b] = tile([P, PASSES, PACK, P], U8, f"wa_s{b}")
+            nc.vector.tensor_copy(
+                out=wa_s[b][:],
+                in_=wa_s_raw[:, :, b * K_PASS : (b + 1) * K_PASS].rearrange("p a (m t) -> p a t m", t=PACK),
+            )
+
         def art_scores(b, t):
             if t == 0:
                 b_rel[b] = tile([P, PACK, S], F32, f"b_rel{b}")
             bank = work.tile([P, S], F32, name="bank")
-            c0 = t * (H // PACK) + b * P
             for a in range(PASSES):
                 nc.tensor.matmul_mx(
                     out=bank[:],
                     lhsT=wa_w[b][:, a, t, :].bitcast(FP8X4),
-                    lhsT_scale=wa_s[a][:, c0 : c0 + P],
+                    lhsT_scale=wa_s[b][:, a, t, :],
                     rhs=art_w[a][:].bitcast(FP4X4),
                     rhs_scale=v_s[a][:, 0:S],
                     start=(a == 0),
@@ -187,33 +186,43 @@ def tile_list_provenance_claim_readout_kernel(
                         start=(a == 0 and t == 0),
                         stop=(a == PASSES - 1 and t == PACK - 1),
                     )
-            h_bf[b, jq] = tile([P, P, PACK], BF16, f"h_bf{b}{jq}")
+            if jq == 0:
+                h_bf[b] = tile([P, S, PACK], BF16, f"h_bf{b}")
             nc.vector.tensor_tensor(
-                h_bf[b, jq][:].rearrange("p (c i) t -> p c t i", i=4),
+                h_bf[b][:, cols, :].rearrange("p (c i) t -> p c t i", i=4),
                 bank[:].rearrange("p (t c i) -> p c t i", t=PACK, i=4),
                 b_rel[b][:, :, cols].rearrange("p t (c i) -> p c t i", i=4),
                 MULT,
             )
 
-        def readout(b, jq):
-            h_w = tile([P, P], I32, f"h_w{b}{jq}")
-            h_s = tile([P, P], U8, f"h_s{b}{jq}")
+        def readout(b, j0, j1):
+            width = (j1 - j0) * P
+            h_w = tile([P, width], I32, f"h_w{b}{j0}")
+            h_s = tile([P, width], U8, f"h_s{b}{j0}")
             nc.vector.quantize_mx(
-                out=h_w[:].bitcast(FP8X4), scales=h_s[:], in_=h_bf[b, jq][:].rearrange("p j t -> p (j t)")
+                out=h_w[:].bitcast(FP8X4),
+                scales=h_s[:],
+                in_=h_bf[b][:, j0 * P : j1 * P, :].rearrange("p j t -> p (j t)"),
             )
-            for n in range(N_TILES):
-                nc.tensor.matmul_mx(
-                    out=acc[jq][:, n, :],
-                    lhsT=wr_w[:, b, 2 * P * n : 2 * P * (n + 1)].bitcast(FP4X4),
-                    lhsT_scale=wr_s[:, b, P * n : P * (n + 1)],
-                    rhs=h_w[:].bitcast(FP8X4),
-                    rhs_scale=h_s[:],
-                    start=(b == 0 and n == 0),
-                    stop=(b == BLOCKS - 1 and n == N_TILES - 1),
-                )
+            for jq in range(j0, j1):
+                cols = slice((jq - j0) * P, (jq - j0 + 1) * P)
+                for n in range(N_TILES):
+                    nc.tensor.matmul_mx(
+                        out=acc[jq][:, n, :],
+                        lhsT=wr_w[:, b, 2 * P * n : 2 * P * (n + 1)].bitcast(FP4X4),
+                        lhsT_scale=wr_s[:, b, P * n : P * (n + 1)],
+                        rhs=h_w[:, cols].bitcast(FP8X4),
+                        rhs_scale=h_s[:, cols],
+                        start=(b == 0 and n == 0),
+                        stop=(b == BLOCKS - 1 and n == N_TILES - 1),
+                    )
             if b == BLOCKS - 1:
+                jq = j0
                 result = tile([P, N_TILES, P], F32, f"result{jq}")
-                nc.scalar.copy(out=result[:], in_=acc[jq][:])
+                if jq == JQ - 1:
+                    nc.vector.tensor_copy(out=result[:], in_=acc[jq][:])
+                else:
+                    nc.scalar.copy(out=result[:], in_=acc[jq][:])
                 nc.sync.dma_start(
                     out=out[:, jq * P : (jq + 1) * P].rearrange("(n p) j -> p n j", p=P), in_=result[:]
                 )
@@ -222,6 +231,8 @@ def tile_list_provenance_claim_readout_kernel(
             round_wo(b, 0)
             round_wo(b, 1)
             order_wa(b)
+            if b > 0:
+                readout(b - 1, 0, JQ)
             quantise_wo(b, 0)
             art_scores(b, 0)
             art_scores(b, 1)
@@ -230,6 +241,6 @@ def tile_list_provenance_claim_readout_kernel(
             art_scores(b, 3)
             for jq in range(JQ):
                 own_scores(b, jq)
-                if jq > 0:
-                    readout(b, jq - 1)
-            readout(b, JQ - 1)
+                if jq > 0 and b == BLOCKS - 1:
+                    readout(b, jq - 1, jq)
+        readout(BLOCKS - 1, JQ - 1, JQ)

@@ -23,7 +23,6 @@ QUADS = 4
 ROWS = 4
 JQ = S // P
 N_TILES = N // P
-HALF = K_PASS // 2
 SHIFT = 16
 
 
@@ -74,12 +73,16 @@ def tile_list_provenance_claim_readout_kernel(
         wa_raw = {}
         rel_sb = {}
 
+        def pieces(b, a):
+            return 2 if (b, a) == (BLOCKS - 1, PASSES - 1) else 1
+
         def load_wo(b, a):
             rows = wo[a * K_PASS : (a + 1) * K_PASS, :].rearrange("(p j) c -> p j c", j=PACK)
-            for h in range(2):
-                wo_raw[b, a, h] = tile([P, PACK, HALF], F32, f"wo_raw{b}{a}{h}")
-                c0 = b * K_PASS + h * HALF
-                nc.sync.dma_start(out=wo_raw[b, a, h][:], in_=rows[:, :, c0 : c0 + HALF])
+            width = K_PASS // pieces(b, a)
+            for h in range(pieces(b, a)):
+                wo_raw[b, a, h] = tile([P, PACK, width], F32, f"wo_raw{b}{a}{h}")
+                c0 = b * K_PASS + h * width
+                nc.sync.dma_start(out=wo_raw[b, a, h][:], in_=rows[:, :, c0 : c0 + width])
 
         def load_wa(b):
             wa_raw[b] = tile([P, PASSES, K_PASS], I32, f"wa_raw{b}")
@@ -105,9 +108,10 @@ def tile_list_provenance_claim_readout_kernel(
             load_wo(b, 0)
             load_rel(b, 0)
             load_wo(b, 1)
+            if b == BLOCKS - 1:
+                load_scales(wr_s, wr_scales)
+                nc.sync.dma_start(out=wr_w[:].bitcast(I32), in_=wr_words.rearrange("a p c -> p a c").bitcast(I32))
             load_rel(b, 1)
-        load_scales(wr_s, wr_scales)
-        nc.sync.dma_start(out=wr_w[:].bitcast(I32), in_=wr_words.rearrange("a p c -> p a c").bitcast(I32))
 
         art_w = [tile([P, S], U16, f"art_w{a}") for a in range(PASSES)]
         own_w = [tile([P, S], U16, f"own_w{a}") for a in range(PASSES)]
@@ -127,8 +131,9 @@ def tile_list_provenance_claim_readout_kernel(
 
         def round_wo(b, a):
             wo_bf[b, a] = tile([P, PACK, P, PACK], BF16, f"wo_bf{b}{a}")
-            for h in range(2):
-                dst = wo_bf[b, a][:, :, h * (P // 2) : (h + 1) * (P // 2), :]
+            width = P // pieces(b, a)
+            for h in range(pieces(b, a)):
+                dst = wo_bf[b, a][:, :, h * width : (h + 1) * width, :]
                 nc.scalar.copy(
                     out=dst.rearrange("p (u w) m j -> p u m j w", w=2),
                     in_=wo_raw[b, a, h][:].rearrange("p j (m u w) -> p u m j w", u=2, w=2),
@@ -189,9 +194,9 @@ def tile_list_provenance_claim_readout_kernel(
             if jq == 0:
                 h_bf[b] = tile([P, S, PACK], BF16, f"h_bf{b}")
             nc.vector.tensor_tensor(
-                h_bf[b][:, cols, :].rearrange("p (c i) t -> p c t i", i=4),
-                bank[:].rearrange("p (t c i) -> p c t i", t=PACK, i=4),
-                b_rel[b][:, :, cols].rearrange("p t (c i) -> p c t i", i=4),
+                h_bf[b][:, cols, :].rearrange("p (c i) t -> p c t i", i=2),
+                bank[:].rearrange("p (t c i) -> p c t i", t=PACK, i=2),
+                b_rel[b][:, :, cols].rearrange("p t (c i) -> p c t i", i=2),
                 MULT,
             )
 

@@ -19,7 +19,6 @@ PACK = 4
 K_PASS = P * PACK
 PASSES = K // K_PASS
 BLOCKS = H // K_PASS
-QUADS = 4
 ROWS = 4
 JQ = S // P
 N_TILES = N // P
@@ -53,15 +52,15 @@ def tile_list_provenance_claim_readout_kernel(
         nc.vector.memset(wr_s[:].rearrange("p a c -> p (a c)").bitcast(I32), 0)
 
         def load_scales(plane, scales):
-            for q in range(QUADS):
+            for r in range(ROWS):
                 nc.sync.dma_start(
-                    out=plane[32 * q : 32 * q + ROWS, :, :].bitcast(I32),
-                    in_=scales[:, ROWS * q : ROWS * (q + 1), :].rearrange("a r c -> r a c").bitcast(I32),
+                    out=plane[r:P:32, :, :].bitcast(I32),
+                    in_=scales[:, r::ROWS, :].rearrange("a q c -> q a c").bitcast(I32),
                 )
 
+        nc.sync.dma_start(out=tab_w[0][:].bitcast(I32), in_=tab_words[0].bitcast(I32))
         nc.sync.dma_start(art_list[:], offs2)
         nc.sync.dma_start(own_list[:], offs)
-        nc.sync.dma_start(out=tab_w[0][:].bitcast(I32), in_=tab_words[0].bitcast(I32))
         for r in range(ROWS):
             nc.sync.dma_start(
                 out=tab_s[r:P:SHIFT, :].bitcast(I32),
@@ -84,15 +83,16 @@ def tile_list_provenance_claim_readout_kernel(
                 c0 = b * K_PASS + h * width
                 nc.sync.dma_start(out=wo_raw[b, a, h][:], in_=rows[:, :, c0 : c0 + width])
 
-        def load_wa(b):
-            wa_raw[b] = tile([P, PASSES, K_PASS], I32, f"wa_raw{b}")
-            words = wa_words.rearrange("a p c i -> p a (c i)").bitcast(I32)
-            nc.sync.dma_start(out=wa_raw[b][:], in_=words[:, :, b * K_PASS : (b + 1) * K_PASS])
+        def load_wa(a):
+            wa_raw[a] = tile([P, H], I32, f"wa_raw{a}")
+            nc.sync.dma_start(out=wa_raw[a][:], in_=wa_words[a].rearrange("p c i -> p (c i)").bitcast(I32))
 
-        def load_rel(b, h):
+        def load_rel(b, t0, t1):
             rows = rel[b * K_PASS : (b + 1) * K_PASS, :].rearrange("(p t) j -> p t j", t=PACK)
-            rel_sb[b, h] = tile([P, 2, S], F32, f"rel{b}{h}")
-            nc.sync.dma_start(out=rel_sb[b, h][:], in_=rows[:, 2 * h : 2 * h + 2, :])
+            piece = tile([P, t1 - t0, S], F32, f"rel{b}{t0}")
+            nc.sync.dma_start(out=piece[:], in_=rows[:, t0:t1, :])
+            for t in range(t0, t1):
+                rel_sb[b, t] = piece[:, t - t0, :]
 
         load_wo(0, 0)
         load_wo(0, 1)
@@ -101,17 +101,17 @@ def tile_list_provenance_claim_readout_kernel(
         nc.sync.dma_start(out=v_s[1][0 : P - SHIFT, :].bitcast(I32), in_=v_s[0][SHIFT:P, :].bitcast(I32))
         load_scales(wa_s_raw, wa_scales)
         load_wa(0)
-        load_rel(0, 0)
-        load_rel(0, 1)
-        for b in range(1, BLOCKS):
-            load_wa(b)
-            load_wo(b, 0)
-            load_rel(b, 0)
-            load_wo(b, 1)
-            if b == BLOCKS - 1:
-                load_scales(wr_s, wr_scales)
-                nc.sync.dma_start(out=wr_w[:].bitcast(I32), in_=wr_words.rearrange("a p c -> p a c").bitcast(I32))
-            load_rel(b, 1)
+        load_wa(1)
+        load_scales(wr_s, wr_scales)
+        load_rel(0, 0, PACK)
+        load_wo(1, 0)
+        load_rel(1, 0, PACK)
+        load_wo(1, 1)
+        load_wo(2, 0)
+        load_rel(2, 0, 2)
+        load_wo(2, 1)
+        nc.sync.dma_start(out=wr_w[:].bitcast(I32), in_=wr_words.rearrange("a p c -> p a c").bitcast(I32))
+        load_rel(2, 2, PACK)
 
         art_w = [tile([P, S], U16, f"art_w{a}") for a in range(PASSES)]
         own_w = [tile([P, S], U16, f"own_w{a}") for a in range(PASSES)]
@@ -148,17 +148,15 @@ def tile_list_provenance_claim_readout_kernel(
                 in_=wo_bf[b, a][:].rearrange("p t m j -> p (t m j)"),
             )
 
-        def order_wa(b):
-            wa_w[b] = tile([P, PASSES, PACK, P], I32, f"wa_w{b}")
-            nc.vector.tensor_copy(
-                out=wa_w[b][:].rearrange("p a t (c i) -> p a c t i", i=4),
-                in_=wa_raw[b][:].rearrange("p a (c i t) -> p a c t i", i=4, t=PACK),
-            )
+        def order_wa_scales(a):
+            wa_s[a] = tile([P, PACK, H // PACK], U8, f"wa_s{a}")
+            nc.vector.tensor_copy(out=wa_s[a][:], in_=wa_s_raw[:, a, :].rearrange("p (m t) -> p t m", t=PACK))
 
-            wa_s[b] = tile([P, PASSES, PACK, P], U8, f"wa_s{b}")
+        def order_wa_words(a):
+            wa_w[a] = tile([P, PACK, H // PACK], I32, f"wa_w{a}")
             nc.vector.tensor_copy(
-                out=wa_s[b][:],
-                in_=wa_s_raw[:, :, b * K_PASS : (b + 1) * K_PASS].rearrange("p a (m t) -> p a t m", t=PACK),
+                out=wa_w[a][:].rearrange("p t (c i) -> p c t i", i=4),
+                in_=wa_raw[a][:].rearrange("p (c i t) -> p c t i", i=4, t=PACK),
             )
 
         def art_scores(b, t):
@@ -168,14 +166,14 @@ def tile_list_provenance_claim_readout_kernel(
             for a in range(PASSES):
                 nc.tensor.matmul_mx(
                     out=bank[:],
-                    lhsT=wa_w[b][:, a, t, :].bitcast(FP8X4),
-                    lhsT_scale=wa_s[b][:, a, t, :],
+                    lhsT=wa_w[a][:, t, b * P : (b + 1) * P].bitcast(FP8X4),
+                    lhsT_scale=wa_s[a][:, t, b * P : (b + 1) * P],
                     rhs=art_w[a][:].bitcast(FP4X4),
                     rhs_scale=v_s[a][:, 0:S],
                     start=(a == 0),
                     stop=(a == PASSES - 1),
                 )
-            nc.vector.tensor_tensor(b_rel[b][:, t, :], bank[:], rel_sb[b, t // 2][:, t % 2, :], MULT)
+            nc.vector.tensor_tensor(b_rel[b][:, t, :], bank[:], rel_sb[b, t], MULT)
 
         def own_scores(b, jq):
             bank = work.tile([P, S], F32, name="bank")
@@ -235,15 +233,23 @@ def tile_list_provenance_claim_readout_kernel(
         for b in range(BLOCKS):
             round_wo(b, 0)
             round_wo(b, 1)
-            order_wa(b)
             if b > 0:
                 readout(b - 1, 0, JQ)
             quantise_wo(b, 0)
+            if b == 0:
+                order_wa_scales(0)
+                order_wa_scales(1)
+                quantise_wo(b, 1)
+                order_wa_words(0)
+                order_wa_words(1)
             art_scores(b, 0)
             art_scores(b, 1)
-            quantise_wo(b, 1)
+            if b == BLOCKS - 1:
+                quantise_wo(b, 1)
             art_scores(b, 2)
             art_scores(b, 3)
+            if 0 < b < BLOCKS - 1:
+                quantise_wo(b, 1)
             for jq in range(JQ):
                 own_scores(b, jq)
                 if jq > 0 and b == BLOCKS - 1:

@@ -42,38 +42,34 @@ def tile_list_provenance_claim_readout_kernel(
         tab_w = [tile([P, T], U16, f"tab_w{a}") for a in range(PASSES)]
         tab_s = tile([P, T], U8, "tab_s")
         v_s = [tile([P, 2 * S], U8, f"v_s{a}") for a in range(PASSES)]
-        wa_s_raw = tile([P, PASSES, H], U8, "wa_s_raw")
+        wa_s_raw = tile([P, H], U8, "wa_s_raw")
+        wa_s = [tile([P, PACK, H // PACK], U8, f"wa_s{a}") for a in range(PASSES)]
         wr_w = tile([P, BLOCKS, 2 * N], U8, "wr_w")
         wr_s = tile([P, BLOCKS, N], U8, "wr_s")
 
         nc.vector.memset(tab_s[:].bitcast(I32), 0)
-        nc.vector.memset(wa_s_raw[:].rearrange("p a c -> p (a c)").bitcast(I32), 0)
+        nc.vector.memset(wa_s_raw[:].bitcast(I32), 0)
         nc.vector.memset(v_s[1][:].bitcast(I32), 0)
+        nc.vector.memset(wa_s[1][:].rearrange("p t m -> p (t m)").bitcast(I32), 0)
         nc.vector.memset(wr_s[:].rearrange("p a c -> p (a c)").bitcast(I32), 0)
 
-        def load_scales(plane, scales):
+        def load_two_passes(plane, scales):
             for r in range(ROWS):
                 nc.sync.dma_start(
-                    out=plane[r:P:32, :, :].bitcast(I32),
+                    out=plane[r:P:SHIFT, :].bitcast(I32),
                     in_=scales[:, r::ROWS, :].rearrange("a q c -> q a c").bitcast(I32),
                 )
 
-        nc.sync.dma_start(out=tab_w[0][:].bitcast(I32), in_=tab_words[0].bitcast(I32))
-        nc.sync.dma_start(art_list[:], offs2)
-        nc.sync.dma_start(own_list[:], offs)
-        for r in range(ROWS):
-            nc.sync.dma_start(
-                out=tab_s[r:P:SHIFT, :].bitcast(I32),
-                in_=tab_scales[:, r::ROWS, :].rearrange("a q c -> q a c").bitcast(I32),
-            )
-        nc.sync.dma_start(out=tab_w[1][:].bitcast(I32), in_=tab_words[1].bitcast(I32))
+        def lift_second_pass(dst, src):
+            nc.scalar.dma_start(out=dst[0 : P - SHIFT, :].bitcast(I32), in_=src[SHIFT:P, :].bitcast(I32))
 
         wo_raw = {}
         wa_raw = {}
         rel_sb = {}
+        LAST = BLOCKS - 1
 
         def pieces(b, a):
-            return 2 if (b, a) == (BLOCKS - 1, PASSES - 1) else 1
+            return 2 if b == LAST else 1
 
         def load_wo(b, a):
             rows = wo[a * K_PASS : (a + 1) * K_PASS, :].rearrange("(p j) c -> p j c", j=PACK)
@@ -87,40 +83,55 @@ def tile_list_provenance_claim_readout_kernel(
             wa_raw[a] = tile([P, H], I32, f"wa_raw{a}")
             nc.sync.dma_start(out=wa_raw[a][:], in_=wa_words[a].rearrange("p c i -> p (c i)").bitcast(I32))
 
-        def load_rel(b, t0, t1):
+        def load_rel(b, j0, j1):
             rows = rel[b * K_PASS : (b + 1) * K_PASS, :].rearrange("(p t) j -> p t j", t=PACK)
-            piece = tile([P, t1 - t0, S], F32, f"rel{b}{t0}")
-            nc.sync.dma_start(out=piece[:], in_=rows[:, t0:t1, :])
-            for t in range(t0, t1):
-                rel_sb[b, t] = piece[:, t - t0, :]
+            piece = tile([P, PACK, (j1 - j0) * P], F32, f"rel{b}{j0}")
+            nc.sync.dma_start(out=piece[:], in_=rows[:, :, j0 * P : j1 * P])
+            rel_sb[b] = piece
+            for jq in range(j0, j1):
+                rel_sb[b, jq] = piece[:, :, (jq - j0) * P : (jq - j0 + 1) * P]
 
-        load_wo(0, 0)
-        load_wo(0, 1)
-        nc.vector.tensor_copy(v_s[0][:, 0:S], tab_s[:].indirect(art_list[:]))
-        nc.vector.tensor_copy(v_s[0][:, S : 2 * S], tab_s[:].indirect(own_list[:]))
-        nc.sync.dma_start(out=v_s[1][0 : P - SHIFT, :].bitcast(I32), in_=v_s[0][SHIFT:P, :].bitcast(I32))
-        load_scales(wa_s_raw, wa_scales)
+        warm = tile([P, 8], F32, "warm")
+        warm_out = tile([P, 8], BF16, "warm_out")
+        nc.gpsimd.memset(warm[:], 0.0)
+        nc.scalar.copy(out=warm_out[:], in_=warm[:])
+
+        nc.sync.dma_start(art_list[:], offs2)
+        nc.sync.dma_start(out=tab_w[0][:].bitcast(I32), in_=tab_words[0].bitcast(I32))
+        load_two_passes(tab_s, tab_scales)
+        nc.sync.dma_start(out=tab_w[1][:].bitcast(I32), in_=tab_words[1].bitcast(I32))
+        load_two_passes(wa_s_raw, wa_scales)
+        nc.sync.dma_start(own_list[:], offs)
         load_wa(0)
         load_wa(1)
-        load_scales(wr_s, wr_scales)
-        load_rel(0, 0, PACK)
-        load_wo(1, 0)
-        load_rel(1, 0, PACK)
-        load_wo(1, 1)
-        load_wo(2, 0)
-        load_rel(2, 0, 2)
-        load_wo(2, 1)
+        for b in range(LAST):
+            load_wo(b, 0)
+            load_wo(b, 1)
+            load_rel(b, 0, JQ)
+        load_wo(LAST, 0)
+        for r in range(ROWS):
+            nc.sync.dma_start(
+                out=wr_s[r:P:32, :, :].bitcast(I32),
+                in_=wr_scales[:, r::ROWS, :].rearrange("a q c -> q a c").bitcast(I32),
+            )
         nc.sync.dma_start(out=wr_w[:].bitcast(I32), in_=wr_words.rearrange("a p c -> p a c").bitcast(I32))
-        load_rel(2, 2, PACK)
+        load_wo(LAST, 1)
+        load_rel(LAST, 0, 2)
+        load_rel(LAST, 2, 3)
+        load_rel(LAST, 3, 4)
 
         art_w = [tile([P, S], U16, f"art_w{a}") for a in range(PASSES)]
         own_w = [tile([P, S], U16, f"own_w{a}") for a in range(PASSES)]
+        nc.vector.tensor_copy(v_s[0][:, 0:S], tab_s[:].indirect(art_list[:]))
         for a in range(PASSES):
             nc.vector.tensor_copy(art_w[a][:], tab_w[a][:].indirect(art_list[:]))
+        nc.vector.tensor_copy(out=wa_s[0][:], in_=wa_s_raw[:].rearrange("p (m t) -> p t m", t=PACK))
+        lift_second_pass(wa_s[1][:].rearrange("p t m -> p (t m)"), wa_s[0][:].rearrange("p t m -> p (t m)"))
+        nc.vector.tensor_copy(v_s[0][:, S : 2 * S], tab_s[:].indirect(own_list[:]))
+        lift_second_pass(v_s[1], v_s[0])
         for a in range(PASSES):
             nc.vector.tensor_copy(own_w[a][:], tab_w[a][:].indirect(own_list[:]))
 
-        wa_s = {}
         wo_bf = {}
         wo_w = {}
         wo_s = {}
@@ -148,20 +159,19 @@ def tile_list_provenance_claim_readout_kernel(
                 in_=wo_bf[b, a][:].rearrange("p t m j -> p (t m j)"),
             )
 
-        def order_wa_scales(a):
-            wa_s[a] = tile([P, PACK, H // PACK], U8, f"wa_s{a}")
-            nc.vector.tensor_copy(out=wa_s[a][:], in_=wa_s_raw[:, a, :].rearrange("p (m t) -> p t m", t=PACK))
-
         def order_wa_words(a):
             wa_w[a] = tile([P, PACK, H // PACK], I32, f"wa_w{a}")
             nc.vector.tensor_copy(
-                out=wa_w[a][:].rearrange("p t (c i) -> p c t i", i=4),
-                in_=wa_raw[a][:].rearrange("p (c i t) -> p c t i", i=4, t=PACK),
+                out=wa_w[a][:].rearrange("p t m -> p m t"),
+                in_=wa_raw[a][:].rearrange("p (m t) -> p m t", t=PACK),
             )
 
         def art_scores(b, t):
             if t == 0:
-                b_rel[b] = tile([P, PACK, S], F32, f"b_rel{b}")
+                whole = tile([P, PACK, S], F32, f"b_rel{b}")
+                b_rel[b] = whole
+                for jq in range(JQ):
+                    b_rel[b, jq] = whole[:, :, jq * P : (jq + 1) * P]
             bank = work.tile([P, S], F32, name="bank")
             for a in range(PASSES):
                 nc.tensor.matmul_mx(
@@ -173,7 +183,27 @@ def tile_list_provenance_claim_readout_kernel(
                     start=(a == 0),
                     stop=(a == PASSES - 1),
                 )
-            nc.vector.tensor_tensor(b_rel[b][:, t, :], bank[:], rel_sb[b, t], MULT)
+            nc.vector.tensor_tensor(b_rel[b][:, t, :], bank[:], rel_sb[b][:, t, :], MULT)
+
+        def art_scores_quarter(b, jq):
+            bank = work.tile([P, S], F32, name="bank")
+            cols = slice(jq * P, (jq + 1) * P)
+            for a in range(PASSES):
+                for t in range(PACK):
+                    nc.tensor.matmul_mx(
+                        out=bank[:, t * P : (t + 1) * P],
+                        lhsT=wa_w[a][:, t, b * P : (b + 1) * P].bitcast(FP8X4),
+                        lhsT_scale=wa_s[a][:, t, b * P : (b + 1) * P],
+                        rhs=art_w[a][:, cols].bitcast(FP4X4),
+                        rhs_scale=v_s[a][:, cols],
+                        start=(a == 0 and t == 0),
+                        stop=(a == PASSES - 1 and t == PACK - 1),
+                    )
+            quarter = tile([P, PACK, P], F32, f"b_rel{b}{jq}")
+            b_rel[b, jq] = quarter[:]
+            nc.vector.tensor_tensor(
+                quarter[:], bank[:].rearrange("p (t j) -> p t j", t=PACK), rel_sb[b, jq], MULT
+            )
 
         def own_scores(b, jq):
             bank = work.tile([P, S], F32, name="bank")
@@ -194,7 +224,7 @@ def tile_list_provenance_claim_readout_kernel(
             nc.vector.tensor_tensor(
                 h_bf[b][:, cols, :].rearrange("p (c i) t -> p c t i", i=2),
                 bank[:].rearrange("p (t c i) -> p c t i", t=PACK, i=2),
-                b_rel[b][:, :, cols].rearrange("p t (c i) -> p c t i", i=2),
+                b_rel[b, jq].rearrange("p t (c i) -> p c t i", i=2),
                 MULT,
             )
 
@@ -230,28 +260,29 @@ def tile_list_provenance_claim_readout_kernel(
                     out=out[:, jq * P : (jq + 1) * P].rearrange("(n p) j -> p n j", p=P), in_=result[:]
                 )
 
-        for b in range(BLOCKS):
+        order_wa_words(0)
+        order_wa_words(1)
+        for b in range(LAST):
             round_wo(b, 0)
             round_wo(b, 1)
-            if b > 0:
-                readout(b - 1, 0, JQ)
             quantise_wo(b, 0)
-            if b == 0:
-                order_wa_scales(0)
-                order_wa_scales(1)
-                quantise_wo(b, 1)
-                order_wa_words(0)
-                order_wa_words(1)
-            art_scores(b, 0)
-            art_scores(b, 1)
-            if b == BLOCKS - 1:
-                quantise_wo(b, 1)
-            art_scores(b, 2)
-            art_scores(b, 3)
-            if 0 < b < BLOCKS - 1:
-                quantise_wo(b, 1)
+            quantise_wo(b, 1)
+            for t in range(PACK):
+                art_scores(b, t)
             for jq in range(JQ):
                 own_scores(b, jq)
-                if jq > 0 and b == BLOCKS - 1:
-                    readout(b, jq - 1, jq)
-        readout(BLOCKS - 1, JQ - 1, JQ)
+        round_wo(LAST, 0)
+        round_wo(LAST, 1)
+        quantise_wo(LAST, 0)
+        for b in range(LAST):
+            readout(b, 0, JQ)
+        art_scores_quarter(LAST, 0)
+        quantise_wo(LAST, 1)
+        art_scores_quarter(LAST, 1)
+        for jq in range(JQ):
+            own_scores(LAST, jq)
+            if jq + 2 < JQ:
+                art_scores_quarter(LAST, jq + 2)
+            if jq > 0:
+                readout(LAST, jq - 1, jq)
+        readout(LAST, JQ - 1, JQ)

@@ -31,7 +31,7 @@ def tile_list_provenance_claim_readout_kernel(
     nc = tc.nc
     with ExitStack() as ctx:
         keep = ctx.enter_context(tc.tile_pool(name="keep", bufs=1))
-        work = ctx.enter_context(tc.psum_pool(name="work", bufs=4))
+        work = ctx.enter_context(tc.psum_pool(name="work", bufs=1))
         sums = ctx.enter_context(tc.psum_pool(name="sums", bufs=1))
 
         def tile(shape, dtype, name):
@@ -42,15 +42,13 @@ def tile_list_provenance_claim_readout_kernel(
         tab_w = [tile([P, T], U16, f"tab_w{a}") for a in range(PASSES)]
         tab_s = tile([P, T], U8, "tab_s")
         v_s = [tile([P, 2 * S], U8, f"v_s{a}") for a in range(PASSES)]
-        wa_s_raw = tile([P, H], U8, "wa_s_raw")
-        wa_s = [tile([P, PACK, H // PACK], U8, f"wa_s{a}") for a in range(PASSES)]
+        wa_s_raw = tile([P, PASSES, H], U8, "wa_s_raw")
         wr_w = tile([P, BLOCKS, 2 * N], U8, "wr_w")
         wr_s = tile([P, BLOCKS, N], U8, "wr_s")
 
         nc.vector.memset(tab_s[:].bitcast(I32), 0)
-        nc.vector.memset(wa_s_raw[:].bitcast(I32), 0)
+        nc.vector.memset(wa_s_raw[:].rearrange("p a c -> p (a c)").bitcast(I32), 0)
         nc.vector.memset(v_s[1][:].bitcast(I32), 0)
-        nc.vector.memset(wa_s[1][:].rearrange("p t m -> p (t m)").bitcast(I32), 0)
         nc.vector.memset(wr_s[:].rearrange("p a c -> p (a c)").bitcast(I32), 0)
 
         def load_two_passes(plane, scales):
@@ -61,7 +59,7 @@ def tile_list_provenance_claim_readout_kernel(
                 )
 
         def lift_second_pass(dst, src):
-            nc.scalar.dma_start(out=dst[0 : P - SHIFT, :].bitcast(I32), in_=src[SHIFT:P, :].bitcast(I32))
+            nc.sync.dma_start(out=dst[0 : P - SHIFT, :].bitcast(I32), in_=src[SHIFT:P, :].bitcast(I32))
 
         wo_raw = {}
         wa_raw = {}
@@ -79,9 +77,10 @@ def tile_list_provenance_claim_readout_kernel(
                 c0 = b * K_PASS + h * width
                 nc.sync.dma_start(out=wo_raw[b, a, h][:], in_=rows[:, :, c0 : c0 + width])
 
-        def load_wa(a):
-            wa_raw[a] = tile([P, H], I32, f"wa_raw{a}")
-            nc.sync.dma_start(out=wa_raw[a][:], in_=wa_words[a].rearrange("p c i -> p (c i)").bitcast(I32))
+        def load_wa(b):
+            wa_raw[b] = tile([P, PASSES, K_PASS], I32, f"wa_raw{b}")
+            words = wa_words.rearrange("a p c i -> p a (c i)").bitcast(I32)
+            nc.sync.dma_start(out=wa_raw[b][:], in_=words[:, :, b * K_PASS : (b + 1) * K_PASS])
 
         def load_rel(b, j0, j1):
             rows = rel[b * K_PASS : (b + 1) * K_PASS, :].rearrange("(p t) j -> p t j", t=PACK)
@@ -91,29 +90,36 @@ def tile_list_provenance_claim_readout_kernel(
             for jq in range(j0, j1):
                 rel_sb[b, jq] = piece[:, :, (jq - j0) * P : (jq - j0 + 1) * P]
 
-        warm = tile([P, 8], F32, "warm")
-        warm_out = tile([P, 8], BF16, "warm_out")
-        nc.gpsimd.memset(warm[:], 0.0)
-        nc.scalar.copy(out=warm_out[:], in_=warm[:])
+        def load_scales(plane, scales):
+            for r in range(ROWS):
+                nc.sync.dma_start(
+                    out=plane[r:P:32, :, :].bitcast(I32),
+                    in_=scales[:, r::ROWS, :].rearrange("a q c -> q a c").bitcast(I32),
+                )
 
+        def load_tab(a):
+            nc.sync.dma_start(out=tab_w[a][:].bitcast(I32), in_=tab_words[a].bitcast(I32))
+
+        load_tab(0)
         nc.sync.dma_start(art_list[:], offs2)
-        nc.sync.dma_start(out=tab_w[0][:].bitcast(I32), in_=tab_words[0].bitcast(I32))
-        load_two_passes(tab_s, tab_scales)
-        nc.sync.dma_start(out=tab_w[1][:].bitcast(I32), in_=tab_words[1].bitcast(I32))
-        load_two_passes(wa_s_raw, wa_scales)
         nc.sync.dma_start(own_list[:], offs)
+        load_two_passes(tab_s, tab_scales)
+        load_wo(0, 0)
+        load_tab(1)
+        load_scales(wa_s_raw, wa_scales)
         load_wa(0)
+        load_wo(0, 1)
+        nc.vector.tensor_copy(v_s[0][:, 0:S], tab_s[:].indirect(art_list[:]))
+        nc.vector.tensor_copy(v_s[0][:, S : 2 * S], tab_s[:].indirect(own_list[:]))
+        lift_second_pass(v_s[1], v_s[0])
+        load_rel(0, 0, JQ)
         load_wa(1)
-        for b in range(LAST):
-            load_wo(b, 0)
-            load_wo(b, 1)
-            load_rel(b, 0, JQ)
+        load_rel(1, 0, JQ)
+        load_wo(1, 0)
+        load_wo(1, 1)
+        load_wa(2)
         load_wo(LAST, 0)
-        for r in range(ROWS):
-            nc.sync.dma_start(
-                out=wr_s[r:P:32, :, :].bitcast(I32),
-                in_=wr_scales[:, r::ROWS, :].rearrange("a q c -> q a c").bitcast(I32),
-            )
+        load_scales(wr_s, wr_scales)
         nc.sync.dma_start(out=wr_w[:].bitcast(I32), in_=wr_words.rearrange("a p c -> p a c").bitcast(I32))
         load_wo(LAST, 1)
         load_rel(LAST, 0, 2)
@@ -122,13 +128,8 @@ def tile_list_provenance_claim_readout_kernel(
 
         art_w = [tile([P, S], U16, f"art_w{a}") for a in range(PASSES)]
         own_w = [tile([P, S], U16, f"own_w{a}") for a in range(PASSES)]
-        nc.vector.tensor_copy(v_s[0][:, 0:S], tab_s[:].indirect(art_list[:]))
         for a in range(PASSES):
             nc.vector.tensor_copy(art_w[a][:], tab_w[a][:].indirect(art_list[:]))
-        nc.vector.tensor_copy(out=wa_s[0][:], in_=wa_s_raw[:].rearrange("p (m t) -> p t m", t=PACK))
-        lift_second_pass(wa_s[1][:].rearrange("p t m -> p (t m)"), wa_s[0][:].rearrange("p t m -> p (t m)"))
-        nc.vector.tensor_copy(v_s[0][:, S : 2 * S], tab_s[:].indirect(own_list[:]))
-        lift_second_pass(v_s[1], v_s[0])
         for a in range(PASSES):
             nc.vector.tensor_copy(own_w[a][:], tab_w[a][:].indirect(own_list[:]))
 
@@ -137,17 +138,29 @@ def tile_list_provenance_claim_readout_kernel(
         wo_s = {}
         wa_w = {}
         b_rel = {}
+        b_sb = {}
+        h_q = {}
         h_bf = {}
         acc = [sums.tile([P, N_TILES, P], F32, name=f"acc{jq}") for jq in range(JQ)]
 
+        banks_taken = []
+
+        def next_bank():
+            banks_taken.append(0)
+            return work.tile([P, S], F32, name=f"bank{len(banks_taken) % 4}")
+
         def round_wo(b, a):
             wo_bf[b, a] = tile([P, PACK, P, PACK], BF16, f"wo_bf{b}{a}")
-            width = P // pieces(b, a)
-            for h in range(pieces(b, a)):
+            width = P // 2
+            for h in range(2):
                 dst = wo_bf[b, a][:, :, h * width : (h + 1) * width, :]
+                if pieces(b, a) == 2:
+                    src = wo_raw[b, a, h][:]
+                else:
+                    src = wo_raw[b, a, 0][:, :, h * PACK * width : (h + 1) * PACK * width]
                 nc.scalar.copy(
                     out=dst.rearrange("p (u w) m j -> p u m j w", w=2),
-                    in_=wo_raw[b, a, h][:].rearrange("p j (m u w) -> p u m j w", u=2, w=2),
+                    in_=src.rearrange("p j (m u w) -> p u m j w", u=2, w=2),
                 )
 
         def quantise_wo(b, a):
@@ -159,12 +172,21 @@ def tile_list_provenance_claim_readout_kernel(
                 in_=wo_bf[b, a][:].rearrange("p t m j -> p (t m j)"),
             )
 
-        def order_wa_words(a):
-            wa_w[a] = tile([P, PACK, H // PACK], I32, f"wa_w{a}")
-            nc.vector.tensor_copy(
-                out=wa_w[a][:].rearrange("p t m -> p m t"),
-                in_=wa_raw[a][:].rearrange("p (m t) -> p m t", t=PACK),
-            )
+        def order_wa_scales(b0, b1):
+            for a in range(PASSES):
+                ordered = tile([P, b1 - b0, PACK, P], U8, f"wa_s{a}{b0}")
+                nc.gpsimd.tensor_copy(
+                    out=ordered[:],
+                    in_=wa_s_raw[:, a, b0 * K_PASS : b1 * K_PASS].rearrange("p (b m t) -> p b t m", m=P, t=PACK),
+                )
+                for b in range(b0, b1):
+                    wa_w["wa_s", b, a] = ordered[:, b - b0, :, :]
+
+        def order_wa_words(b):
+            for a in range(PASSES):
+                ordered = tile([P, PACK, P], I32, f"wa_w{b}{a}")
+                nc.gpsimd.tensor_copy(out=ordered[:], in_=wa_raw[b][:, a, :].rearrange("p (m t) -> p t m", t=PACK))
+                wa_w["wa_w", b, a] = ordered[:]
 
         def art_scores(b, t):
             if t == 0:
@@ -172,12 +194,12 @@ def tile_list_provenance_claim_readout_kernel(
                 b_rel[b] = whole
                 for jq in range(JQ):
                     b_rel[b, jq] = whole[:, :, jq * P : (jq + 1) * P]
-            bank = work.tile([P, S], F32, name="bank")
+            bank = next_bank()
             for a in range(PASSES):
                 nc.tensor.matmul_mx(
                     out=bank[:],
-                    lhsT=wa_w[a][:, t, b * P : (b + 1) * P].bitcast(FP8X4),
-                    lhsT_scale=wa_s[a][:, t, b * P : (b + 1) * P],
+                    lhsT=wa_w["wa_w", b, a][:, t, :].bitcast(FP8X4),
+                    lhsT_scale=wa_w["wa_s", b, a][:, t, :],
                     rhs=art_w[a][:].bitcast(FP4X4),
                     rhs_scale=v_s[a][:, 0:S],
                     start=(a == 0),
@@ -185,28 +207,30 @@ def tile_list_provenance_claim_readout_kernel(
                 )
             nc.vector.tensor_tensor(b_rel[b][:, t, :], bank[:], rel_sb[b][:, t, :], MULT)
 
-        def art_scores_quarter(b, jq):
-            bank = work.tile([P, S], F32, name="bank")
+        def art_bank(b, jq):
+            bank = next_bank()
             cols = slice(jq * P, (jq + 1) * P)
             for a in range(PASSES):
                 for t in range(PACK):
                     nc.tensor.matmul_mx(
                         out=bank[:, t * P : (t + 1) * P],
-                        lhsT=wa_w[a][:, t, b * P : (b + 1) * P].bitcast(FP8X4),
-                        lhsT_scale=wa_s[a][:, t, b * P : (b + 1) * P],
+                        lhsT=wa_w["wa_w", b, a][:, t, :].bitcast(FP8X4),
+                        lhsT_scale=wa_w["wa_s", b, a][:, t, :],
                         rhs=art_w[a][:, cols].bitcast(FP4X4),
                         rhs_scale=v_s[a][:, cols],
                         start=(a == 0 and t == 0),
                         stop=(a == PASSES - 1 and t == PACK - 1),
                     )
+            return bank[:].rearrange("p (t j) -> p t j", t=PACK)
+
+        def relate_on_vector(b, jq):
+            bank = art_bank(b, jq)
             quarter = tile([P, PACK, P], F32, f"b_rel{b}{jq}")
             b_rel[b, jq] = quarter[:]
-            nc.vector.tensor_tensor(
-                quarter[:], bank[:].rearrange("p (t j) -> p t j", t=PACK), rel_sb[b, jq], MULT
-            )
+            nc.vector.tensor_tensor(quarter[:], bank, rel_sb[b, jq], MULT)
 
         def own_scores(b, jq):
-            bank = work.tile([P, S], F32, name="bank")
+            bank = next_bank()
             cols = slice(jq * P, (jq + 1) * P)
             for a in range(PASSES):
                 for t in range(PACK):
@@ -228,7 +252,7 @@ def tile_list_provenance_claim_readout_kernel(
                 MULT,
             )
 
-        def readout(b, j0, j1):
+        def quantise_h(b, j0, j1):
             width = (j1 - j0) * P
             h_w = tile([P, width], I32, f"h_w{b}{j0}")
             h_s = tile([P, width], U8, f"h_s{b}{j0}")
@@ -239,13 +263,17 @@ def tile_list_provenance_claim_readout_kernel(
             )
             for jq in range(j0, j1):
                 cols = slice((jq - j0) * P, (jq - j0 + 1) * P)
+                h_q[b, jq] = (h_w[:, cols], h_s[:, cols])
+
+        def readout(b, j0, j1):
+            for jq in range(j0, j1):
                 for n in range(N_TILES):
                     nc.tensor.matmul_mx(
                         out=acc[jq][:, n, :],
                         lhsT=wr_w[:, b, 2 * P * n : 2 * P * (n + 1)].bitcast(FP4X4),
                         lhsT_scale=wr_s[:, b, P * n : P * (n + 1)],
-                        rhs=h_w[:, cols].bitcast(FP8X4),
-                        rhs_scale=h_s[:, cols],
+                        rhs=h_q[b, jq][0].bitcast(FP8X4),
+                        rhs_scale=h_q[b, jq][1],
                         start=(b == 0 and n == 0),
                         stop=(b == BLOCKS - 1 and n == N_TILES - 1),
                     )
@@ -260,29 +288,42 @@ def tile_list_provenance_claim_readout_kernel(
                     out=out[:, jq * P : (jq + 1) * P].rearrange("(n p) j -> p n j", p=P), in_=result[:]
                 )
 
+        order_wa_scales(0, 1)
         order_wa_words(0)
-        order_wa_words(1)
-        for b in range(LAST):
+        order_wa_scales(1, BLOCKS)
+        for b in range(1, BLOCKS):
+            order_wa_words(b)
+        for b in range(BLOCKS):
             round_wo(b, 0)
             round_wo(b, 1)
-            quantise_wo(b, 0)
-            quantise_wo(b, 1)
-            for t in range(PACK):
-                art_scores(b, t)
-            for jq in range(JQ):
-                own_scores(b, jq)
-        round_wo(LAST, 0)
-        round_wo(LAST, 1)
-        quantise_wo(LAST, 0)
-        for b in range(LAST):
-            readout(b, 0, JQ)
-        art_scores_quarter(LAST, 0)
-        quantise_wo(LAST, 1)
-        art_scores_quarter(LAST, 1)
+
+        quantise_wo(0, 0)
+        quantise_wo(0, 1)
+        for t in range(PACK):
+            art_scores(0, t)
         for jq in range(JQ):
-            own_scores(LAST, jq)
+            own_scores(0, jq)
+        art_scores(1, 0)
+        quantise_h(0, 0, JQ)
+        for t in range(1, PACK):
+            art_scores(1, t)
+        quantise_wo(1, 0)
+        quantise_wo(1, 1)
+        for jq in range(JQ):
+            own_scores(1, jq)
+        quantise_wo(LAST, 0)
+        quantise_h(1, 0, JQ)
+        for done in range(LAST):
+            readout(done, 0, JQ)
+        relate_on_vector(LAST, 0)
+        quantise_wo(LAST, 1)
+        relate_on_vector(LAST, 1)
+        for jq in range(JQ):
             if jq + 2 < JQ:
-                art_scores_quarter(LAST, jq + 2)
+                relate_on_vector(LAST, jq + 2)
+            own_scores(LAST, jq)
             if jq > 0:
+                quantise_h(LAST, jq - 1, jq)
                 readout(LAST, jq - 1, jq)
+        quantise_h(LAST, JQ - 1, JQ)
         readout(LAST, JQ - 1, JQ)

@@ -115,23 +115,20 @@ def tile_list_provenance_claim_readout_kernel(
         load_rel(0, 0, JQ)
         load_wa(1)
         load_rel(1, 0, JQ)
+        load_scales(wr_s, wr_scales)
+        nc.sync.dma_start(out=wr_w[:].bitcast(I32), in_=wr_words.rearrange("a p c -> p a c").bitcast(I32))
         load_wo(1, 0)
         load_wo(1, 1)
         load_wa(2)
         load_wo(LAST, 0)
-        load_scales(wr_s, wr_scales)
-        nc.sync.dma_start(out=wr_w[:].bitcast(I32), in_=wr_words.rearrange("a p c -> p a c").bitcast(I32))
         load_wo(LAST, 1)
         load_rel(LAST, 0, 2)
         load_rel(LAST, 2, 3)
         load_rel(LAST, 3, 4)
 
         art_w = [tile([P, S], U16, f"art_w{a}") for a in range(PASSES)]
-        own_w = [tile([P, S], U16, f"own_w{a}") for a in range(PASSES)]
         for a in range(PASSES):
             nc.vector.tensor_copy(art_w[a][:], tab_w[a][:].indirect(art_list[:]))
-        for a in range(PASSES):
-            nc.vector.tensor_copy(own_w[a][:], tab_w[a][:].indirect(own_list[:]))
 
         wo_bf = {}
         wo_w = {}
@@ -172,40 +169,23 @@ def tile_list_provenance_claim_readout_kernel(
                 in_=wo_bf[b, a][:].rearrange("p t m j -> p (t m j)"),
             )
 
-        def order_wa_scales(b0, b1):
+        def order_wa_scales(b):
+            ordered = tile([P, PASSES, PACK, P], U8, f"wa_s{b}")
+            nc.vector.tensor_copy(
+                out=ordered[:],
+                in_=wa_s_raw[:, :, b * K_PASS : (b + 1) * K_PASS].rearrange("p a (m t) -> p a t m", t=PACK),
+            )
             for a in range(PASSES):
-                ordered = tile([P, b1 - b0, PACK, P], U8, f"wa_s{a}{b0}")
-                nc.gpsimd.tensor_copy(
-                    out=ordered[:],
-                    in_=wa_s_raw[:, a, b0 * K_PASS : b1 * K_PASS].rearrange("p (b m t) -> p b t m", m=P, t=PACK),
-                )
-                for b in range(b0, b1):
-                    wa_w["wa_s", b, a] = ordered[:, b - b0, :, :]
+                wa_w["wa_s", b, a] = ordered[:, a, :, :]
 
         def order_wa_words(b):
+            ordered = tile([P, PASSES, PACK, P], I32, f"wa_w{b}")
+            nc.vector.tensor_copy(
+                out=ordered[:].rearrange("p a t m -> p a m t"),
+                in_=wa_raw[b][:].rearrange("p a (m t) -> p a m t", t=PACK),
+            )
             for a in range(PASSES):
-                ordered = tile([P, PACK, P], I32, f"wa_w{b}{a}")
-                nc.gpsimd.tensor_copy(out=ordered[:], in_=wa_raw[b][:, a, :].rearrange("p (m t) -> p t m", t=PACK))
-                wa_w["wa_w", b, a] = ordered[:]
-
-        def art_scores(b, t):
-            if t == 0:
-                whole = tile([P, PACK, S], F32, f"b_rel{b}")
-                b_rel[b] = whole
-                for jq in range(JQ):
-                    b_rel[b, jq] = whole[:, :, jq * P : (jq + 1) * P]
-            bank = next_bank()
-            for a in range(PASSES):
-                nc.tensor.matmul_mx(
-                    out=bank[:],
-                    lhsT=wa_w["wa_w", b, a][:, t, :].bitcast(FP8X4),
-                    lhsT_scale=wa_w["wa_s", b, a][:, t, :],
-                    rhs=art_w[a][:].bitcast(FP4X4),
-                    rhs_scale=v_s[a][:, 0:S],
-                    start=(a == 0),
-                    stop=(a == PASSES - 1),
-                )
-            nc.vector.tensor_tensor(b_rel[b][:, t, :], bank[:], rel_sb[b][:, t, :], MULT)
+                wa_w["wa_w", b, a] = ordered[:, a, :, :]
 
         def art_bank(b, jq):
             bank = next_bank()
@@ -221,13 +201,18 @@ def tile_list_provenance_claim_readout_kernel(
                         start=(a == 0 and t == 0),
                         stop=(a == PASSES - 1 and t == PACK - 1),
                     )
-            return bank[:].rearrange("p (t j) -> p t j", t=PACK)
+            return bank
 
         def relate_on_vector(b, jq):
             bank = art_bank(b, jq)
-            quarter = tile([P, PACK, P], F32, f"b_rel{b}{jq}")
+            quarter = tile([P, P, PACK], F32, f"b_rel{b}{jq}")
             b_rel[b, jq] = quarter[:]
-            nc.vector.tensor_tensor(quarter[:], bank, rel_sb[b, jq], MULT)
+            nc.vector.tensor_tensor(
+                quarter[:].rearrange("p (c i) t -> p c t i", i=2),
+                bank[:].rearrange("p (t c i) -> p c t i", t=PACK, i=2),
+                rel_sb[b, jq].rearrange("p t (c i) -> p c t i", i=2),
+                MULT,
+            )
 
         def own_scores(b, jq):
             bank = next_bank()
@@ -238,7 +223,7 @@ def tile_list_provenance_claim_readout_kernel(
                         out=bank[:, t * P : (t + 1) * P],
                         lhsT=wo_w[b, a][:, t * P : (t + 1) * P].bitcast(FP8X4),
                         lhsT_scale=wo_s[b, a][:, t * P : (t + 1) * P],
-                        rhs=own_w[a][:, cols].bitcast(FP4X4),
+                        rhs=own_w[:, a, cols].bitcast(FP4X4),
                         rhs_scale=v_s[a][:, S + jq * P : S + (jq + 1) * P],
                         start=(a == 0 and t == 0),
                         stop=(a == PASSES - 1 and t == PACK - 1),
@@ -246,9 +231,9 @@ def tile_list_provenance_claim_readout_kernel(
             if jq == 0:
                 h_bf[b] = tile([P, S, PACK], BF16, f"h_bf{b}")
             nc.vector.tensor_tensor(
-                h_bf[b][:, cols, :].rearrange("p (c i) t -> p c t i", i=2),
-                bank[:].rearrange("p (t c i) -> p c t i", t=PACK, i=2),
-                b_rel[b, jq].rearrange("p t (c i) -> p c t i", i=2),
+                h_bf[b][:, cols, :],
+                bank[:].rearrange("p (t j) -> p j t", t=PACK),
+                b_rel[b, jq],
                 MULT,
             )
 
@@ -288,33 +273,38 @@ def tile_list_provenance_claim_readout_kernel(
                     out=out[:, jq * P : (jq + 1) * P].rearrange("(n p) j -> p n j", p=P), in_=result[:]
                 )
 
-        order_wa_scales(0, 1)
+        order_wa_scales(0)
         order_wa_words(0)
-        order_wa_scales(1, BLOCKS)
-        for b in range(1, BLOCKS):
-            order_wa_words(b)
+        own_w = tile([P, PASSES, S], U16, "wa_raw0")
+        for a in range(PASSES):
+            nc.vector.tensor_copy(own_w[:, a, :], tab_w[a][:].indirect(own_list[:]))
         for b in range(BLOCKS):
             round_wo(b, 0)
             round_wo(b, 1)
 
         quantise_wo(0, 0)
+        order_wa_scales(1)
         quantise_wo(0, 1)
-        for t in range(PACK):
-            art_scores(0, t)
+        for jq in range(JQ):
+            relate_on_vector(0, jq)
+        order_wa_words(1)
         for jq in range(JQ):
             own_scores(0, jq)
-        art_scores(1, 0)
+        relate_on_vector(1, 0)
         quantise_h(0, 0, JQ)
-        for t in range(1, PACK):
-            art_scores(1, t)
+        readout(0, 0, JQ)
+        relate_on_vector(1, 1)
         quantise_wo(1, 0)
+        relate_on_vector(1, 2)
+        order_wa_scales(2)
+        relate_on_vector(1, 3)
         quantise_wo(1, 1)
+        order_wa_words(2)
         for jq in range(JQ):
             own_scores(1, jq)
         quantise_wo(LAST, 0)
         quantise_h(1, 0, JQ)
-        for done in range(LAST):
-            readout(done, 0, JQ)
+        readout(1, 0, JQ)
         relate_on_vector(LAST, 0)
         quantise_wo(LAST, 1)
         relate_on_vector(LAST, 1)

@@ -67,7 +67,7 @@ def tile_list_provenance_claim_readout_kernel(
         LAST = BLOCKS - 1
 
         def pieces(b, a):
-            return 2 if b == LAST else 1
+            return 2 if (b, a) == (LAST, PASSES - 1) else 1
 
         def load_wo(b, a):
             rows = wo[a * K_PASS : (a + 1) * K_PASS, :].rearrange("(p j) c -> p j c", j=PACK)
@@ -123,8 +123,7 @@ def tile_list_provenance_claim_readout_kernel(
         load_wo(LAST, 0)
         load_wo(LAST, 1)
         load_rel(LAST, 0, 2)
-        load_rel(LAST, 2, 3)
-        load_rel(LAST, 3, 4)
+        load_rel(LAST, 2, 4)
 
         art_w = [tile([P, S], U16, f"art_w{a}") for a in range(PASSES)]
         for a in range(PASSES):
@@ -181,13 +180,32 @@ def tile_list_provenance_claim_readout_kernel(
         def order_wa_words(b):
             ordered = tile([P, PASSES, PACK, P], I32, f"wa_w{b}")
             nc.vector.tensor_copy(
-                out=ordered[:].rearrange("p a t m -> p a m t"),
-                in_=wa_raw[b][:].rearrange("p a (m t) -> p a m t", t=PACK),
+                out=ordered[:].rearrange("p a t (c i) -> p a c t i", i=4),
+                in_=wa_raw[b][:].rearrange("p a (c i t) -> p a c t i", i=4, t=PACK),
             )
             for a in range(PASSES):
                 wa_w["wa_w", b, a] = ordered[:, a, :, :]
 
-        def art_bank(b, jq):
+        def art_scores(b, t):
+            if t == 0:
+                whole = tile([P, PACK, S], F32, f"b_rel{b}")
+                b_rel[b] = whole
+                for jq in range(JQ):
+                    b_rel[b, jq] = whole[:, :, jq * P : (jq + 1) * P]
+            bank = next_bank()
+            for a in range(PASSES):
+                nc.tensor.matmul_mx(
+                    out=bank[:],
+                    lhsT=wa_w["wa_w", b, a][:, t, :].bitcast(FP8X4),
+                    lhsT_scale=wa_w["wa_s", b, a][:, t, :],
+                    rhs=art_w[a][:].bitcast(FP4X4),
+                    rhs_scale=v_s[a][:, 0:S],
+                    start=(a == 0),
+                    stop=(a == PASSES - 1),
+                )
+            nc.vector.tensor_tensor(b_rel[b][:, t, :], bank[:], rel_sb[b][:, t, :], MULT)
+
+        def art_scores_quarter(b, jq):
             bank = next_bank()
             cols = slice(jq * P, (jq + 1) * P)
             for a in range(PASSES):
@@ -201,17 +219,10 @@ def tile_list_provenance_claim_readout_kernel(
                         start=(a == 0 and t == 0),
                         stop=(a == PASSES - 1 and t == PACK - 1),
                     )
-            return bank
-
-        def relate_on_vector(b, jq):
-            bank = art_bank(b, jq)
-            quarter = tile([P, P, PACK], F32, f"b_rel{b}{jq}")
+            quarter = tile([P, PACK, P], F32, f"b_rel{b}{jq}")
             b_rel[b, jq] = quarter[:]
             nc.vector.tensor_tensor(
-                quarter[:].rearrange("p (c i) t -> p c t i", i=2),
-                bank[:].rearrange("p (t c i) -> p c t i", t=PACK, i=2),
-                rel_sb[b, jq].rearrange("p t (c i) -> p c t i", i=2),
-                MULT,
+                quarter[:], bank[:].rearrange("p (t j) -> p t j", t=PACK), rel_sb[b, jq], MULT
             )
 
         def own_scores(b, jq):
@@ -231,9 +242,9 @@ def tile_list_provenance_claim_readout_kernel(
             if jq == 0:
                 h_bf[b] = tile([P, S, PACK], BF16, f"h_bf{b}")
             nc.vector.tensor_tensor(
-                h_bf[b][:, cols, :],
-                bank[:].rearrange("p (t j) -> p j t", t=PACK),
-                b_rel[b, jq],
+                h_bf[b][:, cols, :].rearrange("p (c i) t -> p c t i", i=2),
+                bank[:].rearrange("p (t c i) -> p c t i", t=PACK, i=2),
+                b_rel[b, jq].rearrange("p t (c i) -> p c t i", i=2),
                 MULT,
             )
 
@@ -286,18 +297,18 @@ def tile_list_provenance_claim_readout_kernel(
         order_wa_scales(1)
         quantise_wo(0, 1)
         for jq in range(JQ):
-            relate_on_vector(0, jq)
+            art_scores(0, jq)
         order_wa_words(1)
         for jq in range(JQ):
             own_scores(0, jq)
-        relate_on_vector(1, 0)
+        art_scores(1, 0)
         quantise_h(0, 0, JQ)
         readout(0, 0, JQ)
-        relate_on_vector(1, 1)
+        art_scores(1, 1)
         quantise_wo(1, 0)
-        relate_on_vector(1, 2)
+        art_scores(1, 2)
         order_wa_scales(2)
-        relate_on_vector(1, 3)
+        art_scores(1, 3)
         quantise_wo(1, 1)
         order_wa_words(2)
         for jq in range(JQ):
@@ -305,12 +316,12 @@ def tile_list_provenance_claim_readout_kernel(
         quantise_wo(LAST, 0)
         quantise_h(1, 0, JQ)
         readout(1, 0, JQ)
-        relate_on_vector(LAST, 0)
+        art_scores_quarter(LAST, 0)
         quantise_wo(LAST, 1)
-        relate_on_vector(LAST, 1)
+        art_scores_quarter(LAST, 1)
         for jq in range(JQ):
             if jq + 2 < JQ:
-                relate_on_vector(LAST, jq + 2)
+                art_scores_quarter(LAST, jq + 2)
             own_scores(LAST, jq)
             if jq > 0:
                 quantise_h(LAST, jq - 1, jq)

@@ -113,14 +113,14 @@ def tile_list_provenance_claim_readout_kernel(
         nc.vector.tensor_copy(v_s[0][:, S : 2 * S], tab_s[:].indirect(own_list[:]))
         lift_second_pass(v_s[1], v_s[0])
         load_rel(0, 0, JQ)
+        load_wo(1, 0)
         load_wa(1)
-        load_rel(1, 0, JQ)
         load_scales(wr_s, wr_scales)
         nc.sync.dma_start(out=wr_w[:].bitcast(I32), in_=wr_words.rearrange("a p c -> p a c").bitcast(I32))
-        load_wo(1, 0)
         load_wo(1, 1)
-        load_wa(2)
+        load_rel(1, 0, JQ)
         load_wo(LAST, 0)
+        load_wa(2)
         load_wo(LAST, 1)
         load_rel(LAST, 0, 2)
         load_rel(LAST, 2, 4)
@@ -160,7 +160,7 @@ def tile_list_provenance_claim_readout_kernel(
                 )
 
         def quantise_wo(b, a):
-            wo_w[b, a] = tile([P, K_PASS], I32, f"wo_w{b}{a}")
+            wo_w[b, a] = tile([P, K_PASS], I32, "tab_w0" if (b, a) == (0, 0) else f"wo_w{b}{a}")
             wo_s[b, a] = tile([P, K_PASS], U8, f"wo_s{b}{a}")
             nc.vector.quantize_mx(
                 out=wo_w[b, a][:].bitcast(FP8X4),
@@ -295,33 +295,39 @@ def tile_list_provenance_claim_readout_kernel(
 
         quantise_wo(0, 0)
         order_wa_scales(1)
+        art_scores(0, 0)
+        art_scores(0, 1)
+        order_wa_scales(2)
+        art_scores(0, 2)
         quantise_wo(0, 1)
-        for jq in range(JQ):
-            art_scores(0, jq)
+        art_scores(0, 3)
+        own_scores(0, 0)
+        own_scores(0, 1)
         order_wa_words(1)
-        for jq in range(JQ):
-            own_scores(0, jq)
-        art_scores(1, 0)
+        own_scores(0, 2)
+        own_scores(0, 3)
+        quantise_wo(1, 0)
         quantise_h(0, 0, JQ)
         readout(0, 0, JQ)
+        art_scores(1, 0)
         art_scores(1, 1)
-        quantise_wo(1, 0)
         art_scores(1, 2)
-        order_wa_scales(2)
-        art_scores(1, 3)
         quantise_wo(1, 1)
+        art_scores(1, 3)
+        own_scores(1, 0)
+        own_scores(1, 1)
         order_wa_words(2)
-        for jq in range(JQ):
-            own_scores(1, jq)
+        own_scores(1, 2)
+        own_scores(1, 3)
         quantise_wo(LAST, 0)
         quantise_h(1, 0, JQ)
         readout(1, 0, JQ)
         art_scores_quarter(LAST, 0)
-        quantise_wo(LAST, 1)
         art_scores_quarter(LAST, 1)
+        art_scores_quarter(LAST, 2)
+        quantise_wo(LAST, 1)
+        art_scores_quarter(LAST, 3)
         for jq in range(JQ):
-            if jq + 2 < JQ:
-                art_scores_quarter(LAST, jq + 2)
             own_scores(LAST, jq)
             if jq > 0:
                 quantise_h(LAST, jq - 1, jq)

@@ -115,8 +115,6 @@ def tile_list_provenance_claim_readout_kernel(
         load_rel(0, 0, JQ)
         load_wo(1, 0)
         load_wa(1)
-        load_scales(wr_s, wr_scales)
-        nc.sync.dma_start(out=wr_w[:].bitcast(I32), in_=wr_words.rearrange("a p c -> p a c").bitcast(I32))
         load_wo(1, 1)
         load_rel(1, 0, JQ)
         load_wo(LAST, 0)
@@ -124,6 +122,8 @@ def tile_list_provenance_claim_readout_kernel(
         load_wo(LAST, 1)
         load_rel(LAST, 0, 2)
         load_rel(LAST, 2, 4)
+        load_scales(wr_s, wr_scales)
+        nc.sync.dma_start(out=wr_w[:].bitcast(I32), in_=wr_words.rearrange("a p c -> p a c").bitcast(I32))
 
         art_w = [tile([P, S], U16, f"art_w{a}") for a in range(PASSES)]
         for a in range(PASSES):
@@ -261,8 +261,8 @@ def tile_list_provenance_claim_readout_kernel(
                 cols = slice((jq - j0) * P, (jq - j0 + 1) * P)
                 h_q[b, jq] = (h_w[:, cols], h_s[:, cols])
 
-        def readout(b, j0, j1):
-            for jq in range(j0, j1):
+        def readout(jq):
+            for b in range(BLOCKS):
                 for n in range(N_TILES):
                     nc.tensor.matmul_mx(
                         out=acc[jq][:, n, :],
@@ -273,16 +273,12 @@ def tile_list_provenance_claim_readout_kernel(
                         start=(b == 0 and n == 0),
                         stop=(b == BLOCKS - 1 and n == N_TILES - 1),
                     )
-            if b == BLOCKS - 1:
-                jq = j0
-                result = tile([P, N_TILES, P], F32, f"result{jq}")
-                if jq == JQ - 1:
-                    nc.vector.tensor_copy(out=result[:], in_=acc[jq][:])
-                else:
-                    nc.scalar.copy(out=result[:], in_=acc[jq][:])
-                nc.sync.dma_start(
-                    out=out[:, jq * P : (jq + 1) * P].rearrange("(n p) j -> p n j", p=P), in_=result[:]
-                )
+            result = tile([P, N_TILES, P], F32, f"result{jq}")
+            if jq == JQ - 1:
+                nc.vector.tensor_copy(out=result[:], in_=acc[jq][:])
+            else:
+                nc.scalar.copy(out=result[:], in_=acc[jq][:])
+            nc.sync.dma_start(out=out[:, jq * P : (jq + 1) * P].rearrange("(n p) j -> p n j", p=P), in_=result[:])
 
         order_wa_scales(0)
         order_wa_words(0)
@@ -308,7 +304,6 @@ def tile_list_provenance_claim_readout_kernel(
         own_scores(0, 3)
         quantise_wo(1, 0)
         quantise_h(0, 0, JQ)
-        readout(0, 0, JQ)
         art_scores(1, 0)
         art_scores(1, 1)
         art_scores(1, 2)
@@ -321,7 +316,6 @@ def tile_list_provenance_claim_readout_kernel(
         own_scores(1, 3)
         quantise_wo(LAST, 0)
         quantise_h(1, 0, JQ)
-        readout(1, 0, JQ)
         art_scores_quarter(LAST, 0)
         art_scores_quarter(LAST, 1)
         art_scores_quarter(LAST, 2)
@@ -331,6 +325,6 @@ def tile_list_provenance_claim_readout_kernel(
             own_scores(LAST, jq)
             if jq > 0:
                 quantise_h(LAST, jq - 1, jq)
-                readout(LAST, jq - 1, jq)
+                readout(jq - 1)
         quantise_h(LAST, JQ - 1, JQ)
-        readout(LAST, JQ - 1, JQ)
+        readout(JQ - 1)

@@ -46,8 +46,8 @@ def tile_list_provenance_claim_readout_kernel(
         wr_w = tile([P, BLOCKS, 2 * N], U8, "wr_w")
         wr_s = tile([P, BLOCKS, N], U8, "wr_s")
 
-        nc.vector.memset(tab_s[:].bitcast(I32), 0)
         nc.vector.memset(wa_s_raw[:].rearrange("p a c -> p (a c)").bitcast(I32), 0)
+        nc.vector.memset(tab_s[:].bitcast(I32), 0)
         nc.vector.memset(v_s[1][:].bitcast(I32), 0)
         nc.vector.memset(wr_s[:].rearrange("p a c -> p (a c)").bitcast(I32), 0)
 
@@ -67,32 +67,40 @@ def tile_list_provenance_claim_readout_kernel(
         LAST = BLOCKS - 1
 
         def pieces(b, a):
-            return 2 if (b, a) == (LAST, PASSES - 1) else 1
+            return 2 if (b, a) in ((2, 0), (2, 1)) else 1
 
-        def load_wo(b, a):
+        def load_wo(b, a, h0=0, h1=2):
             rows = wo[a * K_PASS : (a + 1) * K_PASS, :].rearrange("(p j) c -> p j c", j=PACK)
             width = K_PASS // pieces(b, a)
-            for h in range(pieces(b, a)):
+            for h in range(h0, min(h1, pieces(b, a))):
                 wo_raw[b, a, h] = tile([P, PACK, width], F32, f"wo_raw{b}{a}{h}")
                 c0 = b * K_PASS + h * width
                 nc.sync.dma_start(out=wo_raw[b, a, h][:], in_=rows[:, :, c0 : c0 + width])
 
-        def load_wa(b):
-            wa_raw[b] = tile([P, PASSES, K_PASS], I32, f"wa_raw{b}")
+        def load_wa(b0, b1):
+            piece = tile([P, PASSES, (b1 - b0) * K_PASS], I32, f"wa_raw{b0}")
             words = wa_words.rearrange("a p c i -> p a (c i)").bitcast(I32)
-            nc.sync.dma_start(out=wa_raw[b][:], in_=words[:, :, b * K_PASS : (b + 1) * K_PASS])
+            nc.sync.dma_start(out=piece[:], in_=words[:, :, b0 * K_PASS : b1 * K_PASS])
+            for b in range(b0, b1):
+                wa_raw[b] = piece[:, :, (b - b0) * K_PASS : (b - b0 + 1) * K_PASS]
 
         def load_rel(b, j0, j1):
             rows = rel[b * K_PASS : (b + 1) * K_PASS, :].rearrange("(p t) j -> p t j", t=PACK)
             piece = tile([P, PACK, (j1 - j0) * P], F32, f"rel{b}{j0}")
             nc.sync.dma_start(out=piece[:], in_=rows[:, :, j0 * P : j1 * P])
-            rel_sb[b] = piece
             for jq in range(j0, j1):
                 rel_sb[b, jq] = piece[:, :, (jq - j0) * P : (jq - j0 + 1) * P]
 
-        def load_scales(plane, scales):
-            for r in range(ROWS):
-                nc.sync.dma_start(
+        def load_rel_rows(b, t0, t1):
+            rows = rel[b * K_PASS : (b + 1) * K_PASS, :].rearrange("(p t) j -> p t j", t=PACK)
+            piece = tile([P, t1 - t0, S], F32, f"rel{b}r{t0}")
+            nc.sync.dma_start(out=piece[:], in_=rows[:, t0:t1, :])
+            for t in range(t0, t1):
+                rel_sb[b, "t", t] = piece[:, t - t0, :]
+
+        def load_scales(queue, plane, scales, r0, r1):
+            for r in range(r0, r1):
+                queue.dma_start(
                     out=plane[r:P:32, :, :].bitcast(I32),
                     in_=scales[:, r::ROWS, :].rearrange("a q c -> q a c").bitcast(I32),
                 )
@@ -100,30 +108,32 @@ def tile_list_provenance_claim_readout_kernel(
         def load_tab(a):
             nc.sync.dma_start(out=tab_w[a][:].bitcast(I32), in_=tab_words[a].bitcast(I32))
 
+        load_scales(nc.gpsimd, wa_s_raw, wa_scales, 0, 3)
         load_tab(0)
         nc.sync.dma_start(art_list[:], offs2)
         nc.sync.dma_start(own_list[:], offs)
         load_two_passes(tab_s, tab_scales)
-        load_wo(0, 0)
         load_tab(1)
-        load_scales(wa_s_raw, wa_scales)
-        load_wa(0)
+        load_scales(nc.sync, wa_s_raw, wa_scales, 3, ROWS)
+        load_wo(0, 0)
+        load_wa(0, 1)
         load_wo(0, 1)
         nc.vector.tensor_copy(v_s[0][:, 0:S], tab_s[:].indirect(art_list[:]))
         nc.vector.tensor_copy(v_s[0][:, S : 2 * S], tab_s[:].indirect(own_list[:]))
         lift_second_pass(v_s[1], v_s[0])
-        load_rel(0, 0, JQ)
+        load_rel_rows(0, 0, 4)
+        load_wa(1, 2)
         load_wo(1, 0)
-        load_wa(1)
         load_wo(1, 1)
-        load_rel(1, 0, JQ)
-        load_wo(LAST, 0)
-        load_wa(2)
-        load_wo(LAST, 1)
-        load_rel(LAST, 0, 2)
-        load_rel(LAST, 2, 4)
-        load_scales(wr_s, wr_scales)
+        load_rel_rows(1, 0, 2)
+        load_rel_rows(1, 2, 4)
+        load_wa(2, 3)
+        load_wo(2, 0)
+        load_wo(2, 1)
+        load_rel(2, 0, 2)
+        load_scales(nc.sync, wr_s, wr_scales, 0, ROWS)
         nc.sync.dma_start(out=wr_w[:].bitcast(I32), in_=wr_words.rearrange("a p c -> p a c").bitcast(I32))
+        load_rel(2, 2, 4)
 
         art_w = [tile([P, S], U16, f"art_w{a}") for a in range(PASSES)]
         for a in range(PASSES):
@@ -134,10 +144,10 @@ def tile_list_provenance_claim_readout_kernel(
         wo_s = {}
         wa_w = {}
         b_rel = {}
-        b_sb = {}
         h_q = {}
         h_bf = {}
-        acc = [sums.tile([P, N_TILES, P], F32, name=f"acc{jq}") for jq in range(JQ)]
+        accs = {}
+        shared = []
 
         banks_taken = []
 
@@ -154,13 +164,17 @@ def tile_list_provenance_claim_readout_kernel(
                     src = wo_raw[b, a, h][:]
                 else:
                     src = wo_raw[b, a, 0][:, :, h * PACK * width : (h + 1) * PACK * width]
-                nc.scalar.copy(
-                    out=dst.rearrange("p (u w) m j -> p u m j w", w=2),
-                    in_=src.rearrange("p j (m u w) -> p u m j w", u=2, w=2),
-                )
+                dst = dst.rearrange("p (u w) m j -> p u m j w", w=2)
+                src = src.rearrange("p j (m u w) -> p u m j w", u=2, w=2)
+                if (b, a, h) == (LAST, 1, 1):
+                    shared.append((dst[:, :, width // 2 :], src[:, :, width // 2 :]))
+                    dst, src = dst[:, :, : width // 2], src[:, :, : width // 2]
+                nc.scalar.copy(out=dst, in_=src)
 
         def quantise_wo(b, a):
-            wo_w[b, a] = tile([P, K_PASS], I32, "tab_w0" if (b, a) == (0, 0) else f"wo_w{b}{a}")
+            if (b, a) == (LAST, 1):
+                nc.vector.tensor_copy(out=shared[0][0], in_=shared[0][1])
+            wo_w[b, a] = tile([P, K_PASS], I32, f"wo_w{b}{a}")
             wo_s[b, a] = tile([P, K_PASS], U8, f"wo_s{b}{a}")
             nc.vector.quantize_mx(
                 out=wo_w[b, a][:].bitcast(FP8X4),
@@ -168,20 +182,21 @@ def tile_list_provenance_claim_readout_kernel(
                 in_=wo_bf[b, a][:].rearrange("p t m j -> p (t m j)"),
             )
 
-        def order_wa_scales(b):
-            ordered = tile([P, PASSES, PACK, P], U8, f"wa_s{b}")
+        def order_wa_scales():
+            ordered = tile([P, PASSES * BLOCKS, PACK, P], U8, "tab_s")
             nc.vector.tensor_copy(
                 out=ordered[:],
-                in_=wa_s_raw[:, :, b * K_PASS : (b + 1) * K_PASS].rearrange("p a (m t) -> p a t m", t=PACK),
+                in_=wa_s_raw[:].rearrange("p a (b m t) -> p (a b) t m", b=BLOCKS, t=PACK),
             )
             for a in range(PASSES):
-                wa_w["wa_s", b, a] = ordered[:, a, :, :]
+                for b in range(BLOCKS):
+                    wa_w["wa_s", b, a] = ordered[:, a * BLOCKS + b, :, :]
 
         def order_wa_words(b):
             ordered = tile([P, PASSES, PACK, P], I32, f"wa_w{b}")
             nc.vector.tensor_copy(
                 out=ordered[:].rearrange("p a t (c i) -> p a c t i", i=4),
-                in_=wa_raw[b][:].rearrange("p a (c i t) -> p a c t i", i=4, t=PACK),
+                in_=wa_raw[b].rearrange("p a (c i t) -> p a c t i", i=4, t=PACK),
             )
             for a in range(PASSES):
                 wa_w["wa_w", b, a] = ordered[:, a, :, :]
@@ -203,10 +218,10 @@ def tile_list_provenance_claim_readout_kernel(
                     start=(a == 0),
                     stop=(a == PASSES - 1),
                 )
-            nc.vector.tensor_tensor(b_rel[b][:, t, :], bank[:], rel_sb[b][:, t, :], MULT)
+            nc.vector.tensor_tensor(b_rel[b][:, t, :], bank[:], rel_sb[b, "t", t], MULT)
 
         def art_scores_quarter(b, jq):
-            bank = next_bank()
+            bank = sums.tile([P, S], F32, name=f"spare{jq}")
             cols = slice(jq * P, (jq + 1) * P)
             for a in range(PASSES):
                 for t in range(PACK):
@@ -234,7 +249,7 @@ def tile_list_provenance_claim_readout_kernel(
                         out=bank[:, t * P : (t + 1) * P],
                         lhsT=wo_w[b, a][:, t * P : (t + 1) * P].bitcast(FP8X4),
                         lhsT_scale=wo_s[b, a][:, t * P : (t + 1) * P],
-                        rhs=own_w[:, a, cols].bitcast(FP4X4),
+                        rhs=own_w[a][:, cols].bitcast(FP4X4),
                         rhs_scale=v_s[a][:, S + jq * P : S + (jq + 1) * P],
                         start=(a == 0 and t == 0),
                         stop=(a == PASSES - 1 and t == PACK - 1),
@@ -261,11 +276,14 @@ def tile_list_provenance_claim_readout_kernel(
                 cols = slice((jq - j0) * P, (jq - j0 + 1) * P)
                 h_q[b, jq] = (h_w[:, cols], h_s[:, cols])
 
-        def readout(jq):
-            for b in range(BLOCKS):
+        def readout_passes(jq, b0, b1):
+            if b0 == 0:
+                accs[jq] = sums.tile([P, N_TILES, P], F32, name=f"spare{jq}")
+            acc = accs[jq]
+            for b in range(b0, b1):
                 for n in range(N_TILES):
                     nc.tensor.matmul_mx(
-                        out=acc[jq][:, n, :],
+                        out=acc[:, n, :],
                         lhsT=wr_w[:, b, 2 * P * n : 2 * P * (n + 1)].bitcast(FP4X4),
                         lhsT_scale=wr_s[:, b, P * n : P * (n + 1)],
                         rhs=h_q[b, jq][0].bitcast(FP8X4),
@@ -273,29 +291,32 @@ def tile_list_provenance_claim_readout_kernel(
                         start=(b == 0 and n == 0),
                         stop=(b == BLOCKS - 1 and n == N_TILES - 1),
                     )
+
+        def readout(jq):
+            readout_passes(jq, LAST, BLOCKS)
+            acc = accs[jq]
             result = tile([P, N_TILES, P], F32, f"result{jq}")
             if jq == JQ - 1:
-                nc.vector.tensor_copy(out=result[:], in_=acc[jq][:])
+                nc.vector.tensor_copy(out=result[:], in_=acc[:])
             else:
-                nc.scalar.copy(out=result[:], in_=acc[jq][:])
+                nc.scalar.copy(out=result[:], in_=acc[:])
             nc.sync.dma_start(out=out[:, jq * P : (jq + 1) * P].rearrange("(n p) j -> p n j", p=P), in_=result[:])
 
-        order_wa_scales(0)
+        own_w = [tile([P, S], U16, "own_w0")]
+        nc.vector.tensor_copy(own_w[0][:], tab_w[0][:].indirect(own_list[:]))
+        order_wa_scales()
         order_wa_words(0)
-        own_w = tile([P, PASSES, S], U16, "wa_raw0")
-        for a in range(PASSES):
-            nc.vector.tensor_copy(own_w[:, a, :], tab_w[a][:].indirect(own_list[:]))
+        own_w.append(tile([P, S], U16, "wa_raw0"))
+        nc.vector.tensor_copy(own_w[1][:], tab_w[1][:].indirect(own_list[:]))
         for b in range(BLOCKS):
             round_wo(b, 0)
             round_wo(b, 1)
 
         quantise_wo(0, 0)
-        order_wa_scales(1)
         art_scores(0, 0)
         art_scores(0, 1)
-        order_wa_scales(2)
-        art_scores(0, 2)
         quantise_wo(0, 1)
+        art_scores(0, 2)
         art_scores(0, 3)
         own_scores(0, 0)
         own_scores(0, 1)
@@ -303,28 +324,37 @@ def tile_list_provenance_claim_readout_kernel(
         own_scores(0, 2)
         own_scores(0, 3)
         quantise_wo(1, 0)
-        quantise_h(0, 0, JQ)
+        quantise_h(0, 0, 4)
         art_scores(1, 0)
         art_scores(1, 1)
-        art_scores(1, 2)
         quantise_wo(1, 1)
+        art_scores(1, 2)
         art_scores(1, 3)
         own_scores(1, 0)
         own_scores(1, 1)
         order_wa_words(2)
         own_scores(1, 2)
         own_scores(1, 3)
-        quantise_wo(LAST, 0)
-        quantise_h(1, 0, JQ)
-        art_scores_quarter(LAST, 0)
-        art_scores_quarter(LAST, 1)
-        art_scores_quarter(LAST, 2)
-        quantise_wo(LAST, 1)
-        art_scores_quarter(LAST, 3)
-        for jq in range(JQ):
-            own_scores(LAST, jq)
-            if jq > 0:
-                quantise_h(LAST, jq - 1, jq)
-                readout(jq - 1)
-        quantise_h(LAST, JQ - 1, JQ)
-        readout(JQ - 1)
+        quantise_wo(2, 0)
+        quantise_h(1, 0, 4)
+        quantise_wo(2, 1)
+        art_scores_quarter(2, 0)
+        art_scores_quarter(2, 1)
+        own_scores(2, 0)
+        own_scores(2, 1)
+        art_scores_quarter(2, 2)
+        quantise_h(2, 0, 1)
+        art_scores_quarter(2, 3)
+        quantise_h(2, 1, 2)
+        own_scores(2, 2)
+        own_scores(2, 3)
+        quantise_h(2, 2, 3)
+        quantise_h(2, 3, 4)
+        readout_passes(0, 0, LAST)
+        readout(0)
+        readout_passes(1, 0, LAST)
+        readout(1)
+        readout_passes(2, 0, LAST)
+        readout(2)
+        readout_passes(3, 0, LAST)
+        readout(3)

@@ -130,10 +130,10 @@ def tile_list_provenance_claim_readout_kernel(
         load_wa(2, 3)
         load_wo(2, 0)
         load_wo(2, 1)
-        load_rel(2, 0, 2)
         load_scales(nc.sync, wr_s, wr_scales, 0, ROWS)
-        nc.sync.dma_start(out=wr_w[:].bitcast(I32), in_=wr_words.rearrange("a p c -> p a c").bitcast(I32))
+        load_rel(2, 0, 2)
         load_rel(2, 2, 4)
+        nc.sync.dma_start(out=wr_w[:].bitcast(I32), in_=wr_words.rearrange("a p c -> p a c").bitcast(I32))
 
         art_w = [tile([P, S], U16, f"art_w{a}") for a in range(PASSES)]
         for a in range(PASSES):
@@ -167,8 +167,8 @@ def tile_list_provenance_claim_readout_kernel(
                 dst = dst.rearrange("p (u w) m j -> p u m j w", w=2)
                 src = src.rearrange("p j (m u w) -> p u m j w", u=2, w=2)
                 if (b, a, h) == (LAST, 1, 1):
-                    shared.append((dst[:, :, width // 2 :], src[:, :, width // 2 :]))
-                    dst, src = dst[:, :, : width // 2], src[:, :, : width // 2]
+                    shared.append((dst[:, :, 16 :], src[:, :, 16 :]))
+                    dst, src = dst[:, :, : 16], src[:, :, : 16]
                 nc.scalar.copy(out=dst, in_=src)
 
         def quantise_wo(b, a):
@@ -277,30 +277,41 @@ def tile_list_provenance_claim_readout_kernel(
                 h_q[b, jq] = (h_w[:, cols], h_s[:, cols])
 
         def readout_passes(jq, b0, b1):
+            apart = jq == JQ - 1
             if b0 == 0:
-                accs[jq] = sums.tile([P, N_TILES, P], F32, name=f"spare{jq}")
-            acc = accs[jq]
+                if apart:
+                    accs[jq] = [sums.tile([P, P], F32, name=f"spare{jq}")[:]]
+                    accs[jq] += [next_bank()[:, 0:P] for n in range(1, N_TILES)]
+                else:
+                    whole = sums.tile([P, N_TILES, P], F32, name=f"spare{jq}")
+                    accs[jq] = [whole[:, n, :] for n in range(N_TILES)] + [whole[:]]
             for b in range(b0, b1):
                 for n in range(N_TILES):
                     nc.tensor.matmul_mx(
-                        out=acc[:, n, :],
+                        out=accs[jq][n],
                         lhsT=wr_w[:, b, 2 * P * n : 2 * P * (n + 1)].bitcast(FP4X4),
                         lhsT_scale=wr_s[:, b, P * n : P * (n + 1)],
                         rhs=h_q[b, jq][0].bitcast(FP8X4),
                         rhs_scale=h_q[b, jq][1],
-                        start=(b == 0 and n == 0),
-                        stop=(b == BLOCKS - 1 and n == N_TILES - 1),
+                        start=(b == 0 and (apart or n == 0)),
+                        stop=(b == LAST and (apart or n == N_TILES - 1)),
                     )
 
         def readout(jq):
             readout_passes(jq, LAST, BLOCKS)
-            acc = accs[jq]
-            result = tile([P, N_TILES, P], F32, f"result{jq}")
-            if jq == JQ - 1:
-                nc.vector.tensor_copy(out=result[:], in_=acc[:])
-            else:
-                nc.scalar.copy(out=result[:], in_=acc[:])
-            nc.sync.dma_start(out=out[:, jq * P : (jq + 1) * P].rearrange("(n p) j -> p n j", p=P), in_=result[:])
+            cols = slice(jq * P, (jq + 1) * P)
+            if jq < JQ - 1:
+                result = tile([P, N_TILES, P], F32, f"result{jq}")
+                nc.scalar.copy(out=result[:], in_=accs[jq][N_TILES])
+                nc.sync.dma_start(out=out[:, cols].rearrange("(n p) j -> p n j", p=P), in_=result[:])
+                return
+            for n in range(N_TILES):
+                result = tile([P, P], F32, f"result{jq}{n}")
+                if n == 1:
+                    nc.scalar.copy(out=result[:], in_=accs[jq][n])
+                else:
+                    nc.vector.tensor_copy(out=result[:], in_=accs[jq][n])
+                nc.sync.dma_start(out=out[n * P : (n + 1) * P, cols], in_=result[:])
 
         own_w = [tile([P, S], U16, "own_w0")]
         nc.vector.tensor_copy(own_w[0][:], tab_w[0][:].indirect(own_list[:]))
@@ -343,12 +354,11 @@ def tile_list_provenance_claim_readout_kernel(
         own_scores(2, 0)
         own_scores(2, 1)
         art_scores_quarter(2, 2)
-        quantise_h(2, 0, 1)
-        art_scores_quarter(2, 3)
-        quantise_h(2, 1, 2)
+        quantise_h(2, 0, 2)
         own_scores(2, 2)
-        own_scores(2, 3)
+        art_scores_quarter(2, 3)
         quantise_h(2, 2, 3)
+        own_scores(2, 3)
         quantise_h(2, 3, 4)
         readout_passes(0, 0, LAST)
         readout(0)

@@ -18,11 +18,17 @@ P = 128
 PACK = 4
 K_PASS = P * PACK
 PASSES = K // K_PASS
-BLOCKS = H // K_PASS
-ROWS = 4
-JQ = S // P
+GROUPS = H // K_PASS
+LAST = GROUPS - 1
+QUARTERS = S // P
 N_TILES = N // P
+ROWS = 4
 SHIFT = 16
+WORK_BANKS = 4
+HALF = P // 2
+GPSIMD_SCALE_LOADS = 3
+HALVED = ((LAST, 1),)
+SCALAR_KEEPS = {(LAST, 0): 32, (LAST, 1): 24}
 
 
 def tile_list_provenance_claim_readout_kernel(
@@ -43,60 +49,28 @@ def tile_list_provenance_claim_readout_kernel(
         tab_s = tile([P, T], U8, "tab_s")
         v_s = [tile([P, 2 * S], U8, f"v_s{a}") for a in range(PASSES)]
         wa_s_raw = tile([P, PASSES, H], U8, "wa_s_raw")
-        wr_w = tile([P, BLOCKS, 2 * N], U8, "wr_w")
-        wr_s = tile([P, BLOCKS, N], U8, "wr_s")
+        wr_w = tile([P, GROUPS, 2 * N], U8, "wr_w")
+        wr_s = tile([P, GROUPS, N], U8, "wr_s")
 
         nc.vector.memset(wa_s_raw[:].rearrange("p a c -> p (a c)").bitcast(I32), 0)
         nc.vector.memset(tab_s[:].bitcast(I32), 0)
         nc.vector.memset(v_s[1][:].bitcast(I32), 0)
         nc.vector.memset(wr_s[:].rearrange("p a c -> p (a c)").bitcast(I32), 0)
 
-        def load_two_passes(plane, scales):
-            for r in range(ROWS):
-                nc.sync.dma_start(
-                    out=plane[r:P:SHIFT, :].bitcast(I32),
-                    in_=scales[:, r::ROWS, :].rearrange("a q c -> q a c").bitcast(I32),
-                )
-
-        def lift_second_pass(dst, src):
-            nc.sync.dma_start(out=dst[0 : P - SHIFT, :].bitcast(I32), in_=src[SHIFT:P, :].bitcast(I32))
-
         wo_raw = {}
         wa_raw = {}
-        rel_sb = {}
-        LAST = BLOCKS - 1
+        rel_rows = {}
+        rel_quarter = {}
 
-        def pieces(b, a):
-            return 2 if (b, a) in ((2, 0), (2, 1)) else 1
+        def load_tab(a):
+            nc.sync.dma_start(out=tab_w[a][:].bitcast(I32), in_=tab_words[a].bitcast(I32))
 
-        def load_wo(b, a, h0=0, h1=2):
-            rows = wo[a * K_PASS : (a + 1) * K_PASS, :].rearrange("(p j) c -> p j c", j=PACK)
-            width = K_PASS // pieces(b, a)
-            for h in range(h0, min(h1, pieces(b, a))):
-                wo_raw[b, a, h] = tile([P, PACK, width], F32, f"wo_raw{b}{a}{h}")
-                c0 = b * K_PASS + h * width
-                nc.sync.dma_start(out=wo_raw[b, a, h][:], in_=rows[:, :, c0 : c0 + width])
-
-        def load_wa(b0, b1):
-            piece = tile([P, PASSES, (b1 - b0) * K_PASS], I32, f"wa_raw{b0}")
-            words = wa_words.rearrange("a p c i -> p a (c i)").bitcast(I32)
-            nc.sync.dma_start(out=piece[:], in_=words[:, :, b0 * K_PASS : b1 * K_PASS])
-            for b in range(b0, b1):
-                wa_raw[b] = piece[:, :, (b - b0) * K_PASS : (b - b0 + 1) * K_PASS]
-
-        def load_rel(b, j0, j1):
-            rows = rel[b * K_PASS : (b + 1) * K_PASS, :].rearrange("(p t) j -> p t j", t=PACK)
-            piece = tile([P, PACK, (j1 - j0) * P], F32, f"rel{b}{j0}")
-            nc.sync.dma_start(out=piece[:], in_=rows[:, :, j0 * P : j1 * P])
-            for jq in range(j0, j1):
-                rel_sb[b, jq] = piece[:, :, (jq - j0) * P : (jq - j0 + 1) * P]
-
-        def load_rel_rows(b, t0, t1):
-            rows = rel[b * K_PASS : (b + 1) * K_PASS, :].rearrange("(p t) j -> p t j", t=PACK)
-            piece = tile([P, t1 - t0, S], F32, f"rel{b}r{t0}")
-            nc.sync.dma_start(out=piece[:], in_=rows[:, t0:t1, :])
-            for t in range(t0, t1):
-                rel_sb[b, "t", t] = piece[:, t - t0, :]
+        def load_tab_scales():
+            for r in range(ROWS):
+                nc.sync.dma_start(
+                    out=tab_s[r:P:SHIFT, :].bitcast(I32),
+                    in_=tab_scales[:, r::ROWS, :].rearrange("a q c -> q a c").bitcast(I32),
+                )
 
         def load_scales(queue, plane, scales, r0, r1):
             for r in range(r0, r1):
@@ -105,266 +79,257 @@ def tile_list_provenance_claim_readout_kernel(
                     in_=scales[:, r::ROWS, :].rearrange("a q c -> q a c").bitcast(I32),
                 )
 
-        def load_tab(a):
-            nc.sync.dma_start(out=tab_w[a][:].bitcast(I32), in_=tab_words[a].bitcast(I32))
+        def load_wo(g, a):
+            rows = wo[a * K_PASS : (a + 1) * K_PASS, :].rearrange("(p i) c -> p i c", i=PACK)
+            pieces = 2 if (g, a) in HALVED else 1
+            width = K_PASS // pieces
+            for n in range(pieces):
+                piece = tile([P, PACK, width], F32, f"wo_raw{g}{a}{n}")
+                c0 = g * K_PASS + n * width
+                nc.sync.dma_start(out=piece[:], in_=rows[:, :, c0 : c0 + width])
+                for half in range(2 // pieces):
+                    wo_raw[g, a, n + half] = piece[:, :, half * PACK * HALF : (half + 1) * PACK * HALF]
 
-        load_scales(nc.gpsimd, wa_s_raw, wa_scales, 0, 3)
+        def load_wa(g):
+            wa_raw[g] = tile([P, PASSES, K_PASS], I32, f"wa_raw{g}")
+            words = wa_words.rearrange("a p c i -> p a (c i)").bitcast(I32)
+            nc.sync.dma_start(out=wa_raw[g][:], in_=words[:, :, g * K_PASS : (g + 1) * K_PASS])
+
+        def load_rel_rows(g, t0, t1):
+            rows = rel[g * K_PASS : (g + 1) * K_PASS, :].rearrange("(p t) j -> p t j", t=PACK)
+            piece = tile([P, t1 - t0, S], F32, f"rel{g}t{t0}")
+            nc.sync.dma_start(out=piece[:], in_=rows[:, t0:t1, :])
+            for t in range(t0, t1):
+                rel_rows[g, t] = piece[:, t - t0, :]
+
+        def load_last_rel(q0, q1):
+            rows = rel[LAST * K_PASS :, :].rearrange("(p t) j -> p t j", t=PACK)
+            piece = tile([P, PACK, (q1 - q0) * P], F32, f"rel_last{q0}")
+            nc.sync.dma_start(out=piece[:], in_=rows[:, :, q0 * P : q1 * P])
+            for q in range(q0, q1):
+                rel_quarter[q] = piece[:, :, (q - q0) * P : (q - q0 + 1) * P]
+
+        load_scales(nc.gpsimd, wa_s_raw, wa_scales, 0, GPSIMD_SCALE_LOADS)
         load_tab(0)
         nc.sync.dma_start(art_list[:], offs2)
         nc.sync.dma_start(own_list[:], offs)
-        load_two_passes(tab_s, tab_scales)
+        load_tab_scales()
         load_tab(1)
-        load_scales(nc.sync, wa_s_raw, wa_scales, 3, ROWS)
+        load_scales(nc.sync, wa_s_raw, wa_scales, GPSIMD_SCALE_LOADS, ROWS)
         load_wo(0, 0)
-        load_wa(0, 1)
+        load_wa(0)
         load_wo(0, 1)
         nc.vector.tensor_copy(v_s[0][:, 0:S], tab_s[:].indirect(art_list[:]))
         nc.vector.tensor_copy(v_s[0][:, S : 2 * S], tab_s[:].indirect(own_list[:]))
-        lift_second_pass(v_s[1], v_s[0])
-        load_rel_rows(0, 0, 4)
-        load_wa(1, 2)
+        nc.sync.dma_start(out=v_s[1][0 : P - SHIFT, :].bitcast(I32), in_=v_s[0][SHIFT:P, :].bitcast(I32))
+        load_rel_rows(0, 0, PACK)
+        load_wa(1)
         load_wo(1, 0)
         load_wo(1, 1)
-        load_rel_rows(1, 0, 2)
-        load_rel_rows(1, 2, 4)
-        load_wa(2, 3)
-        load_wo(2, 0)
-        load_wo(2, 1)
+        load_rel_rows(1, 0, PACK // 2)
+        load_rel_rows(1, PACK // 2, PACK)
+        load_wa(LAST)
+        load_wo(LAST, 0)
+        load_wo(LAST, 1)
         load_scales(nc.sync, wr_s, wr_scales, 0, ROWS)
-        load_rel(2, 0, 2)
-        load_rel(2, 2, 4)
-        nc.sync.dma_start(out=wr_w[:].bitcast(I32), in_=wr_words.rearrange("a p c -> p a c").bitcast(I32))
+        load_last_rel(0, QUARTERS // 2)
+        load_last_rel(QUARTERS // 2, QUARTERS)
+        nc.sync.dma_start(out=wr_w[:].bitcast(I32), in_=wr_words.rearrange("g p c -> p g c").bitcast(I32))
 
         art_w = [tile([P, S], U16, f"art_w{a}") for a in range(PASSES)]
         for a in range(PASSES):
             nc.vector.tensor_copy(art_w[a][:], tab_w[a][:].indirect(art_list[:]))
 
         wo_bf = {}
-        wo_w = {}
-        wo_s = {}
-        wa_w = {}
+        left_to_vector = {}
+        wo_q = {}
+        wa_words_q = {}
+        b_rel_whole = {}
         b_rel = {}
-        h_q = {}
         h_bf = {}
-        accs = {}
-        shared = []
-
+        h_q = {}
         banks_taken = []
 
         def next_bank():
             banks_taken.append(0)
-            return work.tile([P, S], F32, name=f"bank{len(banks_taken) % 4}")
+            return work.tile([P, S], F32, name=f"bank{len(banks_taken) % WORK_BANKS}")
 
-        def round_wo(b, a):
-            wo_bf[b, a] = tile([P, PACK, P, PACK], BF16, f"wo_bf{b}{a}")
-            width = P // 2
-            for h in range(2):
-                dst = wo_bf[b, a][:, :, h * width : (h + 1) * width, :]
-                if pieces(b, a) == 2:
-                    src = wo_raw[b, a, h][:]
-                else:
-                    src = wo_raw[b, a, 0][:, :, h * PACK * width : (h + 1) * PACK * width]
-                dst = dst.rearrange("p (u w) m j -> p u m j w", w=2)
-                src = src.rearrange("p j (m u w) -> p u m j w", u=2, w=2)
-                if (b, a, h) == (LAST, 1, 1):
-                    shared.append((dst[:, :, 16 :], src[:, :, 16 :]))
-                    dst, src = dst[:, :, : 16], src[:, :, : 16]
-                nc.scalar.copy(out=dst, in_=src)
+        def round_wo(g, a):
+            wo_bf[g, a] = tile([P, PACK, P, PACK], BF16, f"wo_bf{g}{a}")
+            for half in range(2):
+                dst = wo_bf[g, a][:, :, half * HALF : (half + 1) * HALF, :].rearrange("p (u w) m i -> p u m i w", w=2)
+                src = wo_raw[g, a, half].rearrange("p i (m u w) -> p u m i w", u=2, w=2)
+                mine = SCALAR_KEEPS.get((g, a), HALF) if half == 1 else HALF
+                if mine < HALF:
+                    left_to_vector[g, a] = (dst[:, :, mine:], src[:, :, mine:])
+                nc.scalar.copy(out=dst[:, :, :mine], in_=src[:, :, :mine])
 
-        def quantise_wo(b, a):
-            if (b, a) == (LAST, 1):
-                nc.vector.tensor_copy(out=shared[0][0], in_=shared[0][1])
-            wo_w[b, a] = tile([P, K_PASS], I32, f"wo_w{b}{a}")
-            wo_s[b, a] = tile([P, K_PASS], U8, f"wo_s{b}{a}")
+        def quantise_wo(g, a):
+            if (g, a) in left_to_vector:
+                nc.vector.tensor_copy(out=left_to_vector[g, a][0], in_=left_to_vector[g, a][1])
+            words = tile([P, K_PASS], I32, f"wo_w{g}{a}")
+            plane = tile([P, K_PASS], U8, f"wo_s{g}{a}")
             nc.vector.quantize_mx(
-                out=wo_w[b, a][:].bitcast(FP8X4),
-                scales=wo_s[b, a][:],
-                in_=wo_bf[b, a][:].rearrange("p t m j -> p (t m j)"),
+                out=words[:].bitcast(FP8X4),
+                scales=plane[:],
+                in_=wo_bf[g, a][:].rearrange("p t m i -> p (t m i)"),
             )
+            for t in range(PACK):
+                wo_q[g, a, t] = (words[:, t * P : (t + 1) * P], plane[:, t * P : (t + 1) * P])
 
         def order_wa_scales():
-            ordered = tile([P, PASSES * BLOCKS, PACK, P], U8, "tab_s")
+            ordered = tile([P, PASSES * GROUPS, PACK, P], U8, "tab_s")
             nc.vector.tensor_copy(
                 out=ordered[:],
-                in_=wa_s_raw[:].rearrange("p a (b m t) -> p (a b) t m", b=BLOCKS, t=PACK),
+                in_=wa_s_raw[:].rearrange("p a (g m t) -> p (a g) t m", g=GROUPS, t=PACK),
             )
-            for a in range(PASSES):
-                for b in range(BLOCKS):
-                    wa_w["wa_s", b, a] = ordered[:, a * BLOCKS + b, :, :]
+            return ordered
 
-        def order_wa_words(b):
-            ordered = tile([P, PASSES, PACK, P], I32, f"wa_w{b}")
+        def order_wa_words(g):
+            wa_words_q[g] = tile([P, PASSES, PACK, P], I32, f"wa_w{g}")
             nc.vector.tensor_copy(
-                out=ordered[:].rearrange("p a t (c i) -> p a c t i", i=4),
-                in_=wa_raw[b].rearrange("p a (c i t) -> p a c t i", i=4, t=PACK),
+                out=wa_words_q[g][:].rearrange("p a t (c e) -> p a c t e", e=4),
+                in_=wa_raw[g][:].rearrange("p a (c e t) -> p a c t e", e=4, t=PACK),
             )
-            for a in range(PASSES):
-                wa_w["wa_w", b, a] = ordered[:, a, :, :]
 
-        def art_scores(b, t):
+        def wa_q(g, a, t):
+            return wa_words_q[g][:, a, t, :], wa_planes[:, a * GROUPS + g, t, :]
+
+        def quarter_scores(bank, stationary, moving, plane_col, q):
+            for a in range(PASSES):
+                for t in range(PACK):
+                    words, plane = stationary(a, t)
+                    nc.tensor.matmul_mx(
+                        out=bank[:, t * P : (t + 1) * P],
+                        lhsT=words.bitcast(FP8X4),
+                        lhsT_scale=plane,
+                        rhs=moving[a][:, q * P : (q + 1) * P].bitcast(FP4X4),
+                        rhs_scale=v_s[a][:, plane_col + q * P : plane_col + (q + 1) * P],
+                        start=(a == 0 and t == 0),
+                        stop=(a == PASSES - 1 and t == PACK - 1),
+                    )
+
+        def b_times_rel(g, t):
             if t == 0:
-                whole = tile([P, PACK, S], F32, f"b_rel{b}")
-                b_rel[b] = whole
-                for jq in range(JQ):
-                    b_rel[b, jq] = whole[:, :, jq * P : (jq + 1) * P]
+                b_rel_whole[g] = tile([P, PACK, S], F32, f"b_rel{g}")
+                for q in range(QUARTERS):
+                    b_rel[g, q] = b_rel_whole[g][:, :, q * P : (q + 1) * P]
             bank = next_bank()
             for a in range(PASSES):
+                words, plane = wa_q(g, a, t)
                 nc.tensor.matmul_mx(
                     out=bank[:],
-                    lhsT=wa_w["wa_w", b, a][:, t, :].bitcast(FP8X4),
-                    lhsT_scale=wa_w["wa_s", b, a][:, t, :],
+                    lhsT=words.bitcast(FP8X4),
+                    lhsT_scale=plane,
                     rhs=art_w[a][:].bitcast(FP4X4),
                     rhs_scale=v_s[a][:, 0:S],
                     start=(a == 0),
                     stop=(a == PASSES - 1),
                 )
-            nc.vector.tensor_tensor(b_rel[b][:, t, :], bank[:], rel_sb[b, "t", t], MULT)
+            nc.vector.tensor_tensor(b_rel_whole[g][:, t, :], bank[:], rel_rows[g, t], MULT)
 
-        def art_scores_quarter(b, jq):
-            bank = sums.tile([P, S], F32, name=f"spare{jq}")
-            cols = slice(jq * P, (jq + 1) * P)
-            for a in range(PASSES):
-                for t in range(PACK):
-                    nc.tensor.matmul_mx(
-                        out=bank[:, t * P : (t + 1) * P],
-                        lhsT=wa_w["wa_w", b, a][:, t, :].bitcast(FP8X4),
-                        lhsT_scale=wa_w["wa_s", b, a][:, t, :],
-                        rhs=art_w[a][:, cols].bitcast(FP4X4),
-                        rhs_scale=v_s[a][:, cols],
-                        start=(a == 0 and t == 0),
-                        stop=(a == PASSES - 1 and t == PACK - 1),
-                    )
-            quarter = tile([P, PACK, P], F32, f"b_rel{b}{jq}")
-            b_rel[b, jq] = quarter[:]
-            nc.vector.tensor_tensor(
-                quarter[:], bank[:].rearrange("p (t j) -> p t j", t=PACK), rel_sb[b, jq], MULT
-            )
+        def last_b_times_rel(q):
+            bank = sums.tile([P, S], F32, name=f"spare{q}")
+            quarter_scores(bank, lambda a, t: wa_q(LAST, a, t), art_w, 0, q)
+            product = tile([P, PACK, P], F32, f"b_rel_last{q}")
+            b_rel[LAST, q] = product[:]
+            nc.vector.tensor_tensor(product[:], bank[:].rearrange("p (t j) -> p t j", t=PACK), rel_quarter[q], MULT)
 
-        def own_scores(b, jq):
+        def make_h(g, q):
             bank = next_bank()
-            cols = slice(jq * P, (jq + 1) * P)
-            for a in range(PASSES):
-                for t in range(PACK):
-                    nc.tensor.matmul_mx(
-                        out=bank[:, t * P : (t + 1) * P],
-                        lhsT=wo_w[b, a][:, t * P : (t + 1) * P].bitcast(FP8X4),
-                        lhsT_scale=wo_s[b, a][:, t * P : (t + 1) * P],
-                        rhs=own_w[a][:, cols].bitcast(FP4X4),
-                        rhs_scale=v_s[a][:, S + jq * P : S + (jq + 1) * P],
-                        start=(a == 0 and t == 0),
-                        stop=(a == PASSES - 1 and t == PACK - 1),
-                    )
-            if jq == 0:
-                h_bf[b] = tile([P, S, PACK], BF16, f"h_bf{b}")
+            quarter_scores(bank, lambda a, t: wo_q[g, a, t], own_w, S, q)
+            if q == 0:
+                h_bf[g] = tile([P, S, PACK], BF16, f"h_bf{g}")
             nc.vector.tensor_tensor(
-                h_bf[b][:, cols, :].rearrange("p (c i) t -> p c t i", i=2),
-                bank[:].rearrange("p (t c i) -> p c t i", t=PACK, i=2),
-                b_rel[b, jq].rearrange("p t (c i) -> p c t i", i=2),
+                h_bf[g][:, q * P : (q + 1) * P, :].rearrange("p (c e) t -> p c t e", e=2),
+                bank[:].rearrange("p (t c e) -> p c t e", t=PACK, e=2),
+                b_rel[g, q].rearrange("p t (c e) -> p c t e", e=2),
                 MULT,
             )
 
-        def quantise_h(b, j0, j1):
-            width = (j1 - j0) * P
-            h_w = tile([P, width], I32, f"h_w{b}{j0}")
-            h_s = tile([P, width], U8, f"h_s{b}{j0}")
+        def quantise_h(g, q0, q1):
+            words = tile([P, (q1 - q0) * P], I32, f"h_w{g}{q0}")
+            plane = tile([P, (q1 - q0) * P], U8, f"h_s{g}{q0}")
             nc.vector.quantize_mx(
-                out=h_w[:].bitcast(FP8X4),
-                scales=h_s[:],
-                in_=h_bf[b][:, j0 * P : j1 * P, :].rearrange("p j t -> p (j t)"),
+                out=words[:].bitcast(FP8X4),
+                scales=plane[:],
+                in_=h_bf[g][:, q0 * P : q1 * P, :].rearrange("p j t -> p (j t)"),
             )
-            for jq in range(j0, j1):
-                cols = slice((jq - j0) * P, (jq - j0 + 1) * P)
-                h_q[b, jq] = (h_w[:, cols], h_s[:, cols])
+            for q in range(q0, q1):
+                cols = slice((q - q0) * P, (q - q0 + 1) * P)
+                h_q[g, q] = (words[:, cols], plane[:, cols])
 
-        def readout_passes(jq, b0, b1):
-            apart = jq == JQ - 1
-            if b0 == 0:
-                if apart:
-                    accs[jq] = [sums.tile([P, P], F32, name=f"spare{jq}")[:]]
-                    accs[jq] += [next_bank()[:, 0:P] for n in range(1, N_TILES)]
-                else:
-                    whole = sums.tile([P, N_TILES, P], F32, name=f"spare{jq}")
-                    accs[jq] = [whole[:, n, :] for n in range(N_TILES)] + [whole[:]]
-            for b in range(b0, b1):
+        def readout_passes(q, targets, apart):
+            for g in range(GROUPS):
                 for n in range(N_TILES):
                     nc.tensor.matmul_mx(
-                        out=accs[jq][n],
-                        lhsT=wr_w[:, b, 2 * P * n : 2 * P * (n + 1)].bitcast(FP4X4),
-                        lhsT_scale=wr_s[:, b, P * n : P * (n + 1)],
-                        rhs=h_q[b, jq][0].bitcast(FP8X4),
-                        rhs_scale=h_q[b, jq][1],
-                        start=(b == 0 and (apart or n == 0)),
-                        stop=(b == LAST and (apart or n == N_TILES - 1)),
+                        out=targets[n],
+                        lhsT=wr_w[:, g, 2 * P * n : 2 * P * (n + 1)].bitcast(FP4X4),
+                        lhsT_scale=wr_s[:, g, P * n : P * (n + 1)],
+                        rhs=h_q[g, q][0].bitcast(FP8X4),
+                        rhs_scale=h_q[g, q][1],
+                        start=(g == 0 and (apart or n == 0)),
+                        stop=(g == LAST and (apart or n == N_TILES - 1)),
                     )
 
-        def readout(jq):
-            readout_passes(jq, LAST, BLOCKS)
-            cols = slice(jq * P, (jq + 1) * P)
-            if jq < JQ - 1:
-                result = tile([P, N_TILES, P], F32, f"result{jq}")
-                nc.scalar.copy(out=result[:], in_=accs[jq][N_TILES])
-                nc.sync.dma_start(out=out[:, cols].rearrange("(n p) j -> p n j", p=P), in_=result[:])
-                return
+        def readout(q):
+            bank = sums.tile([P, N_TILES, P], F32, name=f"spare{q}")
+            readout_passes(q, [bank[:, n, :] for n in range(N_TILES)], False)
+            result = tile([P, N_TILES, P], F32, f"result{q}")
+            nc.scalar.copy(out=result[:], in_=bank[:])
+            nc.sync.dma_start(out=out[:, q * P : (q + 1) * P].rearrange("(n p) j -> p n j", p=P), in_=result[:])
+
+        def last_readout():
+            q = QUARTERS - 1
+            targets = [sums.tile([P, P], F32, name=f"spare{q}")[:]]
+            targets.extend([next_bank()[:, 0:P] for n in range(1, N_TILES)])
+            readout_passes(q, targets, True)
             for n in range(N_TILES):
-                result = tile([P, P], F32, f"result{jq}{n}")
-                if n == 1:
-                    nc.scalar.copy(out=result[:], in_=accs[jq][n])
+                result = tile([P, P], F32, f"result{q}{n}")
+                if n % 2 == 1:
+                    nc.scalar.copy(out=result[:], in_=targets[n])
                 else:
-                    nc.vector.tensor_copy(out=result[:], in_=accs[jq][n])
-                nc.sync.dma_start(out=out[n * P : (n + 1) * P, cols], in_=result[:])
+                    nc.vector.tensor_copy(out=result[:], in_=targets[n])
+                nc.sync.dma_start(out=out[n * P : (n + 1) * P, q * P : (q + 1) * P], in_=result[:])
 
         own_w = [tile([P, S], U16, "own_w0")]
         nc.vector.tensor_copy(own_w[0][:], tab_w[0][:].indirect(own_list[:]))
-        order_wa_scales()
+        wa_planes = order_wa_scales()
         order_wa_words(0)
         own_w.append(tile([P, S], U16, "wa_raw0"))
         nc.vector.tensor_copy(own_w[1][:], tab_w[1][:].indirect(own_list[:]))
-        for b in range(BLOCKS):
-            round_wo(b, 0)
-            round_wo(b, 1)
+        for g in range(GROUPS):
+            for a in range(PASSES):
+                round_wo(g, a)
 
         quantise_wo(0, 0)
-        art_scores(0, 0)
-        art_scores(0, 1)
-        quantise_wo(0, 1)
-        art_scores(0, 2)
-        art_scores(0, 3)
-        own_scores(0, 0)
-        own_scores(0, 1)
-        order_wa_words(1)
-        own_scores(0, 2)
-        own_scores(0, 3)
-        quantise_wo(1, 0)
-        quantise_h(0, 0, 4)
-        art_scores(1, 0)
-        art_scores(1, 1)
-        quantise_wo(1, 1)
-        art_scores(1, 2)
-        art_scores(1, 3)
-        own_scores(1, 0)
-        own_scores(1, 1)
-        order_wa_words(2)
-        own_scores(1, 2)
-        own_scores(1, 3)
-        quantise_wo(2, 0)
-        quantise_h(1, 0, 4)
-        quantise_wo(2, 1)
-        art_scores_quarter(2, 0)
-        art_scores_quarter(2, 1)
-        own_scores(2, 0)
-        own_scores(2, 1)
-        art_scores_quarter(2, 2)
-        quantise_h(2, 0, 2)
-        own_scores(2, 2)
-        art_scores_quarter(2, 3)
-        quantise_h(2, 2, 3)
-        own_scores(2, 3)
-        quantise_h(2, 3, 4)
-        readout_passes(0, 0, LAST)
-        readout(0)
-        readout_passes(1, 0, LAST)
-        readout(1)
-        readout_passes(2, 0, LAST)
-        readout(2)
-        readout_passes(3, 0, LAST)
-        readout(3)
+        for g in range(LAST):
+            b_times_rel(g, 0)
+            b_times_rel(g, 1)
+            quantise_wo(g, 1)
+            b_times_rel(g, 2)
+            b_times_rel(g, 3)
+            make_h(g, 0)
+            make_h(g, 1)
+            order_wa_words(g + 1)
+            make_h(g, 2)
+            make_h(g, 3)
+            quantise_wo(g + 1, 0)
+            quantise_h(g, 0, QUARTERS)
+
+        quantise_wo(LAST, 1)
+        last_b_times_rel(0)
+        last_b_times_rel(1)
+        make_h(LAST, 0)
+        make_h(LAST, 1)
+        last_b_times_rel(2)
+        quantise_h(LAST, 0, 1)
+        quantise_h(LAST, 1, 2)
+        make_h(LAST, 2)
+        last_b_times_rel(3)
+        quantise_h(LAST, 2, 3)
+        make_h(LAST, 3)
+        quantise_h(LAST, 3, 4)
+        for q in range(QUARTERS - 1):
+            readout(q)
+        last_readout()

from contextlib import ExitStack

import concourse.mybir as mybir

K, H, N, T, S = 1024, 1536, 384, 2048, 512
FLOPS = 2 * (2 * K * H * S + H * N * S)

F32 = mybir.dt.float32
BF16 = mybir.dt.bfloat16
I32 = mybir.dt.int32
U16 = mybir.dt.uint16
U8 = mybir.dt.uint8
FP8X4 = mybir.dt.float8_e4m3fn_x4
FP4X4 = mybir.dt.float4_e2m1fn_x4
MULT = mybir.AluOpType.mult

P = 128
PACK = 4
K_PASS = P * PACK
PASSES = K // K_PASS
GROUPS = H // K_PASS
LAST = GROUPS - 1
QUARTERS = S // P
N_TILES = N // P
ROWS = 4
SHIFT = 16
WORK_BANKS = 4
HALF = P // 2
GPSIMD_SCALE_LOADS = 3
HALVED = ((LAST, 1),)
SCALAR_KEEPS = {(LAST, 0): 32, (LAST, 1): 24}


def tile_list_provenance_claim_readout_kernel(
    tc, tab_words, tab_scales, offs, offs2, wo, wa_words, wa_scales, rel, wr_words, wr_scales, out
):
    nc = tc.nc
    with ExitStack() as ctx:
        keep = ctx.enter_context(tc.tile_pool(name="keep", bufs=1))
        work = ctx.enter_context(tc.psum_pool(name="work", bufs=1))
        sums = ctx.enter_context(tc.psum_pool(name="sums", bufs=1))

        def tile(shape, dtype, name):
            return keep.tile(shape, dtype, name=name, align_bytes=64)

        own_list = keep.tile([P, S // 16], U16, name="own_list")
        art_list = keep.tile([P, S // 16], U16, name="art_list")
        tab_w = [tile([P, T], U16, f"tab_w{a}") for a in range(PASSES)]
        tab_s = tile([P, T], U8, "tab_s")
        v_s = [tile([P, 2 * S], U8, f"v_s{a}") for a in range(PASSES)]
        wa_s_raw = tile([P, PASSES, H], U8, "wa_s_raw")
        wr_w = tile([P, GROUPS, 2 * N], U8, "wr_w")
        wr_s = tile([P, GROUPS, N], U8, "wr_s")

        nc.vector.memset(wa_s_raw[:].rearrange("p a c -> p (a c)").bitcast(I32), 0)
        nc.vector.memset(tab_s[:].bitcast(I32), 0)
        nc.vector.memset(v_s[1][:].bitcast(I32), 0)
        nc.vector.memset(wr_s[:].rearrange("p a c -> p (a c)").bitcast(I32), 0)

        wo_raw = {}
        wa_raw = {}
        rel_rows = {}
        rel_quarter = {}

        def load_tab(a):
            nc.sync.dma_start(out=tab_w[a][:].bitcast(I32), in_=tab_words[a].bitcast(I32))

        def load_tab_scales():
            for r in range(ROWS):
                nc.sync.dma_start(
                    out=tab_s[r:P:SHIFT, :].bitcast(I32),
                    in_=tab_scales[:, r::ROWS, :].rearrange("a q c -> q a c").bitcast(I32),
                )

        def load_scales(queue, plane, scales, r0, r1):
            for r in range(r0, r1):
                queue.dma_start(
                    out=plane[r:P:32, :, :].bitcast(I32),
                    in_=scales[:, r::ROWS, :].rearrange("a q c -> q a c").bitcast(I32),
                )

        def load_wo(g, a):
            rows = wo[a * K_PASS : (a + 1) * K_PASS, :].rearrange("(p i) c -> p i c", i=PACK)
            pieces = 2 if (g, a) in HALVED else 1
            width = K_PASS // pieces
            for n in range(pieces):
                piece = tile([P, PACK, width], F32, f"wo_raw{g}{a}{n}")
                c0 = g * K_PASS + n * width
                nc.sync.dma_start(out=piece[:], in_=rows[:, :, c0 : c0 + width])
                for half in range(2 // pieces):
                    wo_raw[g, a, n + half] = piece[:, :, half * PACK * HALF : (half + 1) * PACK * HALF]

        def load_wa(g):
            wa_raw[g] = tile([P, PASSES, K_PASS], I32, f"wa_raw{g}")
            words = wa_words.rearrange("a p c i -> p a (c i)").bitcast(I32)
            nc.sync.dma_start(out=wa_raw[g][:], in_=words[:, :, g * K_PASS : (g + 1) * K_PASS])

        def load_rel_rows(g, t0, t1):
            rows = rel[g * K_PASS : (g + 1) * K_PASS, :].rearrange("(p t) j -> p t j", t=PACK)
            piece = tile([P, t1 - t0, S], F32, f"rel{g}t{t0}")
            nc.sync.dma_start(out=piece[:], in_=rows[:, t0:t1, :])
            for t in range(t0, t1):
                rel_rows[g, t] = piece[:, t - t0, :]

        def load_last_rel(q0, q1):
            rows = rel[LAST * K_PASS :, :].rearrange("(p t) j -> p t j", t=PACK)
            piece = tile([P, PACK, (q1 - q0) * P], F32, f"rel_last{q0}")
            nc.sync.dma_start(out=piece[:], in_=rows[:, :, q0 * P : q1 * P])
            for q in range(q0, q1):
                rel_quarter[q] = piece[:, :, (q - q0) * P : (q - q0 + 1) * P]

        load_scales(nc.gpsimd, wa_s_raw, wa_scales, 0, GPSIMD_SCALE_LOADS)
        load_tab(0)
        nc.sync.dma_start(art_list[:], offs2)
        nc.sync.dma_start(own_list[:], offs)
        load_tab_scales()
        load_tab(1)
        load_scales(nc.sync, wa_s_raw, wa_scales, GPSIMD_SCALE_LOADS, ROWS)
        load_wo(0, 0)
        load_wa(0)
        load_wo(0, 1)
        nc.vector.tensor_copy(v_s[0][:, 0:S], tab_s[:].indirect(art_list[:]))
        nc.vector.tensor_copy(v_s[0][:, S : 2 * S], tab_s[:].indirect(own_list[:]))
        nc.sync.dma_start(out=v_s[1][0 : P - SHIFT, :].bitcast(I32), in_=v_s[0][SHIFT:P, :].bitcast(I32))
        load_rel_rows(0, 0, PACK)
        load_wa(1)
        load_wo(1, 0)
        load_wo(1, 1)
        load_rel_rows(1, 0, PACK // 2)
        load_rel_rows(1, PACK // 2, PACK)
        load_wa(LAST)
        load_wo(LAST, 0)
        load_wo(LAST, 1)
        load_scales(nc.sync, wr_s, wr_scales, 0, ROWS)
        load_last_rel(0, QUARTERS // 2)
        load_last_rel(QUARTERS // 2, QUARTERS)
        nc.sync.dma_start(out=wr_w[:].bitcast(I32), in_=wr_words.rearrange("g p c -> p g c").bitcast(I32))

        art_w = [tile([P, S], U16, f"art_w{a}") for a in range(PASSES)]
        for a in range(PASSES):
            nc.vector.tensor_copy(art_w[a][:], tab_w[a][:].indirect(art_list[:]))

        wo_bf = {}
        left_to_vector = {}
        wo_q = {}
        wa_words_q = {}
        b_rel_whole = {}
        b_rel = {}
        h_bf = {}
        h_q = {}
        banks_taken = []

        def next_bank():
            banks_taken.append(0)
            return work.tile([P, S], F32, name=f"bank{len(banks_taken) % WORK_BANKS}")

        def round_wo(g, a):
            wo_bf[g, a] = tile([P, PACK, P, PACK], BF16, f"wo_bf{g}{a}")
            for half in range(2):
                dst = wo_bf[g, a][:, :, half * HALF : (half + 1) * HALF, :].rearrange("p (u w) m i -> p u m i w", w=2)
                src = wo_raw[g, a, half].rearrange("p i (m u w) -> p u m i w", u=2, w=2)
                mine = SCALAR_KEEPS.get((g, a), HALF) if half == 1 else HALF
                if mine < HALF:
                    left_to_vector[g, a] = (dst[:, :, mine:], src[:, :, mine:])
                nc.scalar.copy(out=dst[:, :, :mine], in_=src[:, :, :mine])

        def quantise_wo(g, a):
            if (g, a) in left_to_vector:
                nc.vector.tensor_copy(out=left_to_vector[g, a][0], in_=left_to_vector[g, a][1])
            words = tile([P, K_PASS], I32, f"wo_w{g}{a}")
            plane = tile([P, K_PASS], U8, f"wo_s{g}{a}")
            nc.vector.quantize_mx(
                out=words[:].bitcast(FP8X4),
                scales=plane[:],
                in_=wo_bf[g, a][:].rearrange("p t m i -> p (t m i)"),
            )
            for t in range(PACK):
                wo_q[g, a, t] = (words[:, t * P : (t + 1) * P], plane[:, t * P : (t + 1) * P])

        def order_wa_scales():
            ordered = tile([P, PASSES * GROUPS, PACK, P], U8, "tab_s")
            nc.vector.tensor_copy(
                out=ordered[:],
                in_=wa_s_raw[:].rearrange("p a (g m t) -> p (a g) t m", g=GROUPS, t=PACK),
            )
            return ordered

        def order_wa_words(g):
            wa_words_q[g] = tile([P, PASSES, PACK, P], I32, f"wa_w{g}")
            nc.vector.tensor_copy(
                out=wa_words_q[g][:].rearrange("p a t (c e) -> p a c t e", e=4),
                in_=wa_raw[g][:].rearrange("p a (c e t) -> p a c t e", e=4, t=PACK),
            )

        def wa_q(g, a, t):
            return wa_words_q[g][:, a, t, :], wa_planes[:, a * GROUPS + g, t, :]

        def quarter_scores(bank, stationary, moving, plane_col, q):
            for a in range(PASSES):
                for t in range(PACK):
                    words, plane = stationary(a, t)
                    nc.tensor.matmul_mx(
                        out=bank[:, t * P : (t + 1) * P],
                        lhsT=words.bitcast(FP8X4),
                        lhsT_scale=plane,
                        rhs=moving[a][:, q * P : (q + 1) * P].bitcast(FP4X4),
                        rhs_scale=v_s[a][:, plane_col + q * P : plane_col + (q + 1) * P],
                        start=(a == 0 and t == 0),
                        stop=(a == PASSES - 1 and t == PACK - 1),
                    )

        def b_times_rel(g, t):
            if t == 0:
                b_rel_whole[g] = tile([P, PACK, S], F32, f"b_rel{g}")
                for q in range(QUARTERS):
                    b_rel[g, q] = b_rel_whole[g][:, :, q * P : (q + 1) * P]
            bank = next_bank()
            for a in range(PASSES):
                words, plane = wa_q(g, a, t)
                nc.tensor.matmul_mx(
                    out=bank[:],
                    lhsT=words.bitcast(FP8X4),
                    lhsT_scale=plane,
                    rhs=art_w[a][:].bitcast(FP4X4),
                    rhs_scale=v_s[a][:, 0:S],
                    start=(a == 0),
                    stop=(a == PASSES - 1),
                )
            nc.vector.tensor_tensor(b_rel_whole[g][:, t, :], bank[:], rel_rows[g, t], MULT)

        def last_b_times_rel(q):
            bank = sums.tile([P, S], F32, name=f"spare{q}")
            quarter_scores(bank, lambda a, t: wa_q(LAST, a, t), art_w, 0, q)
            product = tile([P, PACK, P], F32, f"b_rel_last{q}")
            b_rel[LAST, q] = product[:]
            nc.vector.tensor_tensor(product[:], bank[:].rearrange("p (t j) -> p t j", t=PACK), rel_quarter[q], MULT)

        def make_h(g, q):
            bank = next_bank()
            quarter_scores(bank, lambda a, t: wo_q[g, a, t], own_w, S, q)
            if q == 0:
                h_bf[g] = tile([P, S, PACK], BF16, f"h_bf{g}")
            nc.vector.tensor_tensor(
                h_bf[g][:, q * P : (q + 1) * P, :].rearrange("p (c e) t -> p c t e", e=2),
                bank[:].rearrange("p (t c e) -> p c t e", t=PACK, e=2),
                b_rel[g, q].rearrange("p t (c e) -> p c t e", e=2),
                MULT,
            )

        def quantise_h(g, q0, q1):
            words = tile([P, (q1 - q0) * P], I32, f"h_w{g}{q0}")
            plane = tile([P, (q1 - q0) * P], U8, f"h_s{g}{q0}")
            nc.vector.quantize_mx(
                out=words[:].bitcast(FP8X4),
                scales=plane[:],
                in_=h_bf[g][:, q0 * P : q1 * P, :].rearrange("p j t -> p (j t)"),
            )
            for q in range(q0, q1):
                cols = slice((q - q0) * P, (q - q0 + 1) * P)
                h_q[g, q] = (words[:, cols], plane[:, cols])

        def readout_passes(q, targets, apart):
            for g in range(GROUPS):
                for n in range(N_TILES):
                    nc.tensor.matmul_mx(
                        out=targets[n],
                        lhsT=wr_w[:, g, 2 * P * n : 2 * P * (n + 1)].bitcast(FP4X4),
                        lhsT_scale=wr_s[:, g, P * n : P * (n + 1)],
                        rhs=h_q[g, q][0].bitcast(FP8X4),
                        rhs_scale=h_q[g, q][1],
                        start=(g == 0 and (apart or n == 0)),
                        stop=(g == LAST and (apart or n == N_TILES - 1)),
                    )

        def readout(q):
            bank = sums.tile([P, N_TILES, P], F32, name=f"spare{q}")
            readout_passes(q, [bank[:, n, :] for n in range(N_TILES)], False)
            result = tile([P, N_TILES, P], F32, f"result{q}")
            nc.scalar.copy(out=result[:], in_=bank[:])
            nc.sync.dma_start(out=out[:, q * P : (q + 1) * P].rearrange("(n p) j -> p n j", p=P), in_=result[:])

        def last_readout():
            q = QUARTERS - 1
            targets = [sums.tile([P, P], F32, name=f"spare{q}")[:]]
            targets.extend([next_bank()[:, 0:P] for n in range(1, N_TILES)])
            readout_passes(q, targets, True)
            for n in range(N_TILES):
                result = tile([P, P], F32, f"result{q}{n}")
                if n % 2 == 1:
                    nc.scalar.copy(out=result[:], in_=targets[n])
                else:
                    nc.vector.tensor_copy(out=result[:], in_=targets[n])
                nc.sync.dma_start(out=out[n * P : (n + 1) * P, q * P : (q + 1) * P], in_=result[:])

        own_w = [tile([P, S], U16, "own_w0")]
        nc.vector.tensor_copy(own_w[0][:], tab_w[0][:].indirect(own_list[:]))
        wa_planes = order_wa_scales()
        order_wa_words(0)
        own_w.append(tile([P, S], U16, "wa_raw0"))
        nc.vector.tensor_copy(own_w[1][:], tab_w[1][:].indirect(own_list[:]))
        for g in range(GROUPS):
            for a in range(PASSES):
                round_wo(g, a)

        quantise_wo(0, 0)
        for g in range(LAST):
            b_times_rel(g, 0)
            b_times_rel(g, 1)
            quantise_wo(g, 1)
            b_times_rel(g, 2)
            b_times_rel(g, 3)
            make_h(g, 0)
            make_h(g, 1)
            order_wa_words(g + 1)
            make_h(g, 2)
            make_h(g, 3)
            quantise_wo(g + 1, 0)
            quantise_h(g, 0, QUARTERS)

        quantise_wo(LAST, 1)
        last_b_times_rel(0)
        last_b_times_rel(1)
        make_h(LAST, 0)
        make_h(LAST, 1)
        last_b_times_rel(2)
        quantise_h(LAST, 0, 1)
        quantise_h(LAST, 1, 2)
        make_h(LAST, 2)
        last_b_times_rel(3)
        quantise_h(LAST, 2, 3)
        make_h(LAST, 3)
        quantise_h(LAST, 3, 4)
        for q in range(QUARTERS - 1):
            readout(q)
        last_readout()
